import numpy as np
import ml_dtypes


def mxq(x, axis, fmt="e4m3"):
    dtype, down = {"e4m3": (ml_dtypes.float8_e4m3fn, 7), "e5m2": (ml_dtypes.float8_e5m2, 14)}[fmt]
    v = np.moveaxis(np.asarray(x, np.float32).astype(ml_dtypes.bfloat16).astype(np.float64), axis, -1)
    blocks = v.reshape(v.shape[:-1] + (-1, 32))
    amax = np.abs(blocks).max(-1, keepdims=True)
    byte = np.maximum(np.where(amax > 0, np.frexp(amax)[1] - 1 + 127, 0) - down, 1)
    scale = np.exp2(byte - 127.0)
    codes = (blocks / scale).astype(np.float32).astype(dtype).astype(np.float64)
    return np.moveaxis((codes * scale).reshape(v.shape), -1, axis)


WIDE = False


def mx_kscale(k):
    if not WIDE:
        return np.ones(k)
    levels = np.array([10, -10, 5, -5, 0])
    if k % 512:
        return np.exp2(np.random.permutation(np.resize(levels, k // 32))).repeat(32)
    a = np.empty((k // 512, 16))
    for p in range(k // 512):
        a[p, :8] = np.random.permutation(np.resize(levels, 8))
        for g in range(8):
            far = levels[np.abs(levels - a[p, g]) >= 10]
            a[p, g + 8] = far[np.random.randint(len(far))]
    return np.exp2(a.ravel()).repeat(32)


def f64(x):
    return np.asarray(x).astype(np.float64)


def striped(idx):
    return np.tile(idx.reshape(-1, 16).T, (8, 1)).astype(np.uint16)


def unstriped(offs):
    return offs[:16].T.reshape(-1).astype(np.int64)


E2M1 = np.array([0.0, 0.5, 1.0, 1.5, 2.0, 3.0, 4.0, 6.0, -0.0, -0.5, -1.0, -1.5, -2.0, -3.0, -4.0, -6.0])


def pack_weight(w, fmt):
    k, n = w.shape
    w = f64(np.asarray(w, np.float32).astype(ml_dtypes.bfloat16)).reshape(k // 32, 32, n)
    amax = np.abs(w).max(1)
    if fmt == "e4m3":
        byte = np.frexp(amax)[1] - 1 + 127 - 7
    else:
        mant, ex = np.frexp(amax / 6.0)
        byte = np.where(mant > 0.5, ex, ex - 1) + 127
    byte = np.clip(np.where(amax > 0, byte, 1), 1, 254)
    scaled = (w * np.exp2(127.0 - byte)[:, None, :]).reshape(k, n).astype(np.float32)
    by_word = np.ascontiguousarray(scaled.reshape(k // 512, 128, 4, n).transpose(0, 1, 3, 2))
    if fmt == "e4m3":
        words = by_word.astype(ml_dtypes.float8_e4m3fn).view(np.uint8)
    else:
        c = by_word.astype(ml_dtypes.float4_e2m1fn).view(np.uint8) & 0xF
        words = (c[..., 0::2] | (c[..., 1::2] << 4)).reshape(k // 512, 128, 2 * n)
    return np.ascontiguousarray(words), np.ascontiguousarray(byte.astype(np.uint8).reshape(k // 512, 16, n))


def unpack_weight(words, scales, fmt):
    g, _, n = scales.shape
    words = np.ascontiguousarray(words).reshape(g, 128, n, -1)
    if fmt == "e4m3":
        vals = words.view(ml_dtypes.float8_e4m3fn).astype(np.float64)
    else:
        nib = np.empty((g, 128, n, 4), np.uint8)
        nib[..., 0::2] = words & 0xF
        nib[..., 1::2] = words >> 4
        vals = E2M1[nib]
    vals = vals * np.repeat(np.exp2(scales.astype(np.float64) - 127.0), 8, axis=1)[..., None]
    return vals.transpose(0, 1, 3, 2).reshape(g * 512, n)


def gelu(v):
    return 0.5 * v * (1.0 + np.tanh(np.sqrt(2.0 / np.pi) * (v + 0.044715 * v**3)))


K, Q, H, N, T, T2, S = 1024, 512, 1024, 512, 2048, 2048, 1024

def setup_inputs():
    n = np.random.standard_normal
    s = mx_kscale(K)[:, None]
    s2 = mx_kscale(Q)[:, None]
    u = mx_kscale(H)[:, None]
    tab_words, tab_scales = pack_weight(n((K, T)) * s, "e4m3")
    tab2_words, tab2_scales = pack_weight(n((Q, T2)) * s2, "e4m3")
    wb4_words, wb4_scales = pack_weight(-0.7 * n((Q, H)) / np.sqrt(Q) / s2, "e2m1")
    return {
        "tab_words": tab_words, "tab_scales": tab_scales,
        "tab2_words": tab2_words, "tab2_scales": tab2_scales,
        "offs": striped(np.random.permutation(T)[:S]),
        "offs2": striped(np.random.permutation(T2)[:S]),
        "wa": (0.7 * n((K, H)) / np.sqrt(K) / s).astype(np.float32),
        "wb4_words": wb4_words, "wb4_scales": wb4_scales,
        "gT": (n((H, T)) * u).astype(np.float32),
        "wm": (n((H, N)) / np.sqrt(H) / u).astype(np.float32),
        "bm": (0.5 * n(N)).astype(np.float32),
    }

def reference(tab_words, tab_scales, tab2_words, tab2_scales, offs, offs2, wa, wb4_words, wb4_scales, gT, wm, bm):
    v = unpack_weight(tab_words, tab_scales, "e4m3")[:, unstriped(offs)]
    v2 = unpack_weight(tab2_words, tab2_scales, "e4m3")[:, unstriped(offs2)]
    wb = unpack_weight(wb4_words, wb4_scales, "e2m1")
    g = f64(gT)[:, unstriped(offs)]
    d = mxq(f64(wa), 0, "e4m3").T @ v + wb.T @ v2
    h = np.exp(-(d * d)) * g
    return (mxq(f64(wm), 0, "e4m3").T @ mxq(h, 0, "e4m3")) + f64(bm)[:, None]

@@ -1,0 +1,273 @@
+from contextlib import ExitStack
+
+import concourse.mybir as mybir
+
+K, Q, H, N, T, S = 1024, 512, 1024, 512, 2048, 1024
+FLOPS = 2 * S * (K * H + Q * H + H * N)
+
+F32 = mybir.dt.float32
+BF16 = mybir.dt.bfloat16
+I32 = mybir.dt.int32
+U32 = mybir.dt.uint32
+U16 = mybir.dt.uint16
+U8 = mybir.dt.uint8
+FP8X4 = mybir.dt.float8_e4m3fn_x4
+FP4X4 = mybir.dt.float4_e2m1fn_x4
+ACT = mybir.ActivationFunctionType
+ALU = mybir.AluOpType
+
+P = 128
+PACK = 4
+PASS = P * PACK
+HALF = 512
+HALVES = S // HALF
+LIST_COLS = HALF // 16
+
+
+def tile_list_pair_distance_messages_kernel(
+    tc, tab_words, tab_scales, tab2_words, tab2_scales, offs, offs2, wa, wb4_words, wb4_scales, gT, wm, bm, out
+):
+    nc = tc.nc
+    with ExitStack() as ctx:
+        sb = ctx.enter_context(tc.tile_pool(name="sb", bufs=1))
+        ps = ctx.enter_context(tc.psum_pool(name="ps", bufs=1))
+
+        def tiles(name, count, shape, dtype):
+            return [sb.tile(shape, dtype, name="%s%d" % (name, i), align_bytes=64) for i in range(count)]
+
+        atoms = sb.tile([P, S // 16], U16, name="atoms")
+        partners = sb.tile([P, S // 16], U16, name="partners")
+        v_words = tiles("v_words", 2, [P, T], I32)
+        v2_words = sb.tile([P, T], I32, name="v2_words", align_bytes=64)
+        v_scales = sb.tile([P, T // 4], I32, name="v_scales", align_bytes=64)
+        v2_scales = sb.tile([P, T // 4], I32, name="v2_scales", align_bytes=64)
+        wb_words_raw = sb.tile([P, H // 2], I32, name="wb_words_raw", align_bytes=64)
+        wb_scales_raw = sb.tile([P, H // 4], I32, name="wb_scales_raw", align_bytes=64)
+        wb_words = sb.tile([P, 2 * H], U8, name="wb_words", align_bytes=64)
+        wb_scales = sb.tile([P, H], U8, name="wb_scales", align_bytes=64)
+        pick_words = tiles("pick_words", 2, [P, S], U32)
+        pick2_words = sb.tile([P, S], U32, name="pick2_words", align_bytes=64)
+        pick_scales = sb.tile([P, S], U8, name="pick_scales", align_bytes=64)
+        pick2_scales = sb.tile([P, S], U8, name="pick2_scales", align_bytes=64)
+        raw = tiles("raw", 4, [P, PACK, PASS], F32)
+        grouped = tiles("grouped", 3, [P, PACK * PASS], BF16)
+        wa_codes = tiles("wa_codes", 2, [P, H], U32)
+        wa_scales = tiles("wa_scales", 2, [P, H], U8)
+        wm_codes = tiles("wm_codes", 2, [P, N], U32)
+        wm_scales = tiles("wm_scales", 2, [P, N], U8)
+        h_codes = tiles("h_codes", 2, [P, S], U32)
+        h_scales = tiles("h_scales", 2, [P, S], U8)
+        g_rows = tiles("g_rows", 8, [P, T], F32)
+        gauss = tiles("gauss", 8, [P, HALF], F32)
+        h_planes = tiles("h_planes", 4, [P, PACK, HALF], F32)
+        bias = sb.tile([P, PACK], F32, name="bias")
+        warm = sb.tile([P, 2], F32, name="warm")
+        banks = [ps.tile([P, HALF], F32, name="bank%d" % i) for i in range(8)]
+
+        g_view = gT.rearrange("(b p t) c -> b t p c", p=P, t=PACK)
+        out_view = out.rearrange("(p t) j -> t p j", t=PACK)
+        turn = []
+
+        def next_grouped():
+            turn.append(0)
+            return grouped[len(turn) % len(grouped)]
+
+        def cast(engine, dst, src):
+            if engine == "scalar":
+                nc.scalar.copy(dst, src)
+            else:
+                nc.vector.tensor_copy(dst, src)
+
+        def load_words(dst, src):
+            nc.sync.dma_start(dst[:], src.rearrange("p c i -> p (c i)").bitcast(I32))
+
+        def load_scales(dst, src):
+            passes = src.shape[0]
+            for q in range(4):
+                nc.sync.dma_start(dst[32 * q : 32 * q + 4 * passes, :], src[:, 4 * q : 4 * q + 4, :].bitcast(I32))
+
+        def load_weight(dst, w, a, b):
+            rows = w[a * PASS : (a + 1) * PASS, b * PASS : (b + 1) * PASS]
+            nc.sync.dma_start(dst[:], rows.rearrange("(p j) c -> p j c", j=PACK))
+
+        def load_g(b, t):
+            nc.sync.dma_start(g_rows[PACK * b + t][:], g_view[b, t])
+
+        def quantize_weight(src, codes, scales, engines):
+            stage = next_grouped()
+            dst_view = stage[:].rearrange("p (t m j) -> p m j t", t=PACK, j=PACK)
+            src_view = src[:].rearrange("p j (m t) -> p m j t", t=PACK)
+            step = P // len(engines)
+            for i, engine in enumerate(engines):
+                cast(engine, dst_view[:, i * step : (i + 1) * step], src_view[:, i * step : (i + 1) * step])
+            nc.vector.quantize_mx(out=codes.bitcast(FP8X4), scales=scales, in_=stage[:])
+
+        def cols(half):
+            return slice(half * HALF, (half + 1) * HALF)
+
+        def entries(lst, half):
+            return lst[:, half * LIST_COLS : (half + 1) * LIST_COLS]
+
+        def pick(dst, table, dtype, lst, half):
+            nc.vector.tensor_copy(dst[:, cols(half)], table[:].bitcast(dtype).indirect(entries(lst, half)))
+
+        def gaussian(b, t, half):
+            unit = (PACK * b + t) * HALVES + half
+            bank = banks[unit % 8]
+            r = slice(b * PASS + t * P, b * PASS + (t + 1) * P)
+            for a in range(2):
+                nc.tensor.matmul_mx(
+                    bank[:],
+                    lhsT=wa_codes[a][:, r].bitcast(FP8X4),
+                    lhsT_scale=wa_scales[a][:, r],
+                    rhs=pick_words[a][:, cols(half)].bitcast(FP8X4),
+                    rhs_scale=pick_scales[4 * a :, cols(half)],
+                    start=(a == 0),
+                    stop=False,
+                )
+            nc.tensor.matmul_mx(
+                bank[:],
+                lhsT=wb_words[:, 2 * r.start : 2 * r.stop].bitcast(FP4X4),
+                lhsT_scale=wb_scales[:, r],
+                rhs=pick2_words[:, cols(half)].bitcast(FP8X4),
+                rhs_scale=pick2_scales[:, cols(half)],
+                start=False,
+                stop=True,
+            )
+            e = gauss[unit % 8]
+            nc.scalar.activation(e[:], bank[:], ACT.Square)
+            nc.scalar.activation(e[:], e[:], ACT.Exp, scale=-1.0)
+
+        def weigh(b, t, half):
+            unit = (PACK * b + t) * HALVES + half
+            nc.vector.tensor_tensor(
+                h_planes[HALVES * b + half][:, t, :],
+                g_rows[PACK * b + t][:].indirect(entries(atoms, half)),
+                gauss[unit % 8][:],
+                ALU.mult,
+            )
+
+        def quantize_h(b, half, engines):
+            stage = next_grouped()
+            dst_view = stage[:].rearrange("p (c i t) -> p c t i", i=4, t=PACK)
+            src_view = h_planes[HALVES * b + half][:].rearrange("p t (c i) -> p c t i", i=4)
+            step = (HALF // 4) // len(engines)
+            for i, engine in enumerate(engines):
+                cast(engine, dst_view[:, i * step : (i + 1) * step], src_view[:, i * step : (i + 1) * step])
+            nc.vector.quantize_mx(
+                out=h_codes[b][:, cols(half)].bitcast(FP8X4), scales=h_scales[b][:, cols(half)], in_=stage[:]
+            )
+
+        def message_pass(b, half):
+            for t in range(PACK):
+                n = slice(t * P, (t + 1) * P)
+                nc.tensor.matmul_mx(
+                    banks[PACK * half + t][:],
+                    lhsT=wm_codes[b][:, n].bitcast(FP8X4),
+                    lhsT_scale=wm_scales[b][:, n],
+                    rhs=h_codes[b][:, cols(half)].bitcast(FP8X4),
+                    rhs_scale=h_scales[b][:, cols(half)],
+                    start=(b == 0),
+                    stop=(b == 1),
+                )
+
+        def finish(half):
+            for t in range(PACK):
+                staged = gauss[PACK * half + t]
+                bank = banks[PACK * half + t]
+                if half == 0 or t % 2 == 0:
+                    nc.scalar.activation(staged[:], bank[:], ACT.Identity, bias=bias[:, t : t + 1])
+                else:
+                    nc.vector.tensor_scalar(staged[:], bank[:], bias[:, t : t + 1], None, ALU.add)
+                nc.sync.dma_start(out_view[t][:, cols(half)], staged[:])
+
+        SS = ("scalar", "scalar")
+        VV = ("vector",)
+        SV = ("scalar", "vector")
+        SSSV = ("scalar", "scalar", "scalar", "vector")
+        SVVV = ("scalar", "vector", "vector", "vector")
+
+        nc.gpsimd.memset(wb_scales_raw[:], 0)
+        nc.gpsimd.memset(v_scales[:], 0)
+        nc.vector.memset(v2_scales[:], 0)
+        nc.vector.memset(warm[:, 0:1], 0.0)
+        nc.scalar.activation(warm[:, 1:2], warm[:, 0:1], ACT.Exp)
+
+        nc.sync.dma_start(wb_words_raw[:], wb4_words[0].bitcast(I32))
+        load_scales(wb_scales_raw, wb4_scales)
+        nc.sync.dma_start(atoms[:], offs)
+        load_words(v_words[0], tab_words[0])
+        load_scales(v_scales, tab_scales)
+        load_weight(raw[0], wa, 0, 0)
+        nc.sync.dma_start(partners[:], offs2)
+        load_words(v_words[1], tab_words[1])
+        load_scales(v2_scales, tab2_scales)
+        load_weight(raw[1], wa, 1, 0)
+        load_words(v2_words, tab2_words[0])
+        load_weight(raw[2], wa, 0, 1)
+        load_weight(raw[3], wa, 1, 1)
+        for b in range(2):
+            nc.vector.tensor_copy(
+                wb_words[:, 2 * b * PASS : 2 * (b + 1) * PASS].rearrange("p (t m e) -> p t m e", t=PACK, e=2),
+                wb_words_raw[:].bitcast(U8)[:, 2 * b * PASS : 2 * (b + 1) * PASS].rearrange(
+                    "p (m t e) -> p t m e", t=PACK, e=2
+                ),
+            )
+        nc.vector.tensor_copy(
+            wb_scales[:].rearrange("p (b t m) -> p b t m", b=2, t=PACK),
+            wb_scales_raw[:].bitcast(U8).rearrange("p (b m t) -> p b t m", b=2, t=PACK),
+        )
+
+        pick(pick_words[0], v_words[0], U32, atoms, 0)
+        pick(pick_scales, v_scales, U8, atoms, 0)
+        quantize_weight(raw[0], wa_codes[0][:, 0:PASS], wa_scales[0][:, 0:PASS], SS)
+        pick(pick_words[1], v_words[1], U32, atoms, 0)
+        pick(pick2_scales, v2_scales, U8, partners, 0)
+        quantize_weight(raw[1], wa_codes[1][:, 0:PASS], wa_scales[1][:, 0:PASS], SS)
+        pick(pick2_words, v2_words, U32, partners, 0)
+        load_weight(raw[0], wm, 0, 0)
+        load_g(0, 0)
+        load_g(0, 1)
+        load_g(0, 2)
+        load_g(0, 3)
+        nc.sync.dma_start(bias[:], bm.rearrange("(p t) -> p t", t=PACK))
+        load_weight(raw[1], wm, 1, 0)
+        load_g(1, 0)
+        load_g(1, 1)
+        load_g(1, 2)
+        load_g(1, 3)
+
+        for t in range(PACK):
+            gaussian(0, t, 0)
+        pick(pick_words[0], v_words[0], U32, atoms, 1)
+        pick(pick_scales, v_scales, U8, atoms, 1)
+        pick(pick_words[1], v_words[1], U32, atoms, 1)
+        pick(pick2_scales, v2_scales, U8, partners, 1)
+        pick(pick2_words, v2_words, U32, partners, 1)
+        for a in range(2):
+            quantize_weight(raw[2 + a], wa_codes[a][:, PASS:H], wa_scales[a][:, PASS:H], SS)
+        for t in range(PACK):
+            gaussian(0, t, 1)
+        for t in range(PACK):
+            for half in range(HALVES):
+                weigh(0, t, half)
+            for half in range(HALVES):
+                gaussian(1, t, half)
+            if t == 0:
+                quantize_weight(raw[0], wm_codes[0][:], wm_scales[0][:], SS)
+        for t in range(PACK - 1):
+            if t < 2:
+                quantize_h(0, t, (SV, SV)[t])
+            for half in range(HALVES):
+                weigh(1, t, half)
+        quantize_weight(raw[1], wm_codes[1][:], wm_scales[1][:], SS)
+        message_pass(0, 0)
+        message_pass(0, 1)
+        weigh(1, 3, 0)
+        quantize_h(1, 0, SV)
+        message_pass(1, 0)
+        weigh(1, 3, 1)
+        quantize_h(1, 1, SV)
+        finish(0)
+        message_pass(1, 1)
+        finish(1)

@@ -20,8 +20,10 @@ P = 128
 PACK = 4
 PASS = P * PACK
 HALF = 512
-HALVES = S // HALF
-LIST_COLS = HALF // 16
+QUADRANT = 32
+PER_COLUMN = 16
+HALVES = (slice(0, HALF), slice(HALF, S))
+WHOLE = slice(0, S)
 
 
 def tile_list_pair_distance_messages_kernel(
@@ -32,49 +34,47 @@ def tile_list_pair_distance_messages_kernel(
         sb = ctx.enter_context(tc.tile_pool(name="sb", bufs=1))
         ps = ctx.enter_context(tc.psum_pool(name="ps", bufs=1))
 
-        def tiles(name, count, shape, dtype):
-            return [sb.tile(shape, dtype, name="%s%d" % (name, i), align_bytes=64) for i in range(count)]
+        def tile(name, shape, dtype):
+            return sb.tile(shape, dtype, name=name, align_bytes=64)
 
-        atoms = sb.tile([P, S // 16], U16, name="atoms")
-        partners = sb.tile([P, S // 16], U16, name="partners")
+        def tiles(name, count, shape, dtype):
+            return [tile("%s%d" % (name, i), shape, dtype) for i in range(count)]
+
+        atoms = sb.tile([P, S // PER_COLUMN], U16, name="atoms")
+        partners = sb.tile([P, S // PER_COLUMN], U16, name="partners")
         v_words = tiles("v_words", 2, [P, T], I32)
-        v2_words = sb.tile([P, T], I32, name="v2_words", align_bytes=64)
-        v_scales = sb.tile([P, T // 4], I32, name="v_scales", align_bytes=64)
-        v2_scales = sb.tile([P, T // 4], I32, name="v2_scales", align_bytes=64)
-        wb_words_raw = sb.tile([P, H // 2], I32, name="wb_words_raw", align_bytes=64)
-        wb_scales_raw = sb.tile([P, H // 4], I32, name="wb_scales_raw", align_bytes=64)
-        wb_words = sb.tile([P, 2 * H], U8, name="wb_words", align_bytes=64)
-        wb_scales = sb.tile([P, H], U8, name="wb_scales", align_bytes=64)
-        pick_words = tiles("pick_words", 2, [P, S], U32)
-        pick2_words = sb.tile([P, S], U32, name="pick2_words", align_bytes=64)
-        pick_scales = sb.tile([P, S], U8, name="pick_scales", align_bytes=64)
-        pick2_scales = sb.tile([P, S], U8, name="pick2_scales", align_bytes=64)
-        raw = tiles("raw", 4, [P, PACK, PASS], F32)
-        grouped = tiles("grouped", 3, [P, PACK * PASS], BF16)
-        wa_codes = tiles("wa_codes", 2, [P, H], U32)
-        wa_scales = tiles("wa_scales", 2, [P, H], U8)
-        wm_codes = tiles("wm_codes", 2, [P, N], U32)
+        v_scales = tile("v_scales", [P, T // 4], I32)
+        v2_words = tile("v2_words", [P, T], I32)
+        v2_scales = tile("v2_scales", [P, T // 4], I32)
+        wb_words_in = tile("wb_words_in", [P, H // 2], I32)
+        wb_scales_in = tile("wb_scales_in", [P, H // 4], I32)
+        wb_words = tile("wb_words", [P, 2 * H], U8)
+        wb_scales = tile("wb_scales", [P, H], U8)
+        atom_words = tiles("atom_words", 2, [P, S], U32)
+        atom_scales = tile("atom_scales", [P, S], U8)
+        partner_words = tile("partner_words", [P, S], U32)
+        partner_scales = tile("partner_scales", [P, S], U8)
+        weight_in = tiles("weight_in", 4, [P, PACK, PASS], F32)
+        staged_pairs = tiles("staged", 2, [P, 2, PACK * PASS], BF16)
+        staged = [staged_pairs[i // 2][:, i % 2, :] for i in range(4)]
+        wa_words = tiles("wa_words", 2, [P, 2, PASS], U32)
+        wa_scales = tiles("wa_scales", 2, [P, 2, PASS], U8)
+        wm_words = tiles("wm_words", 2, [P, N], U32)
         wm_scales = tiles("wm_scales", 2, [P, N], U8)
-        h_codes = tiles("h_codes", 2, [P, S], U32)
+        h_words = tiles("h_words", 2, [P, S], U32)
         h_scales = tiles("h_scales", 2, [P, S], U8)
-        g_rows = tiles("g_rows", 8, [P, T], F32)
-        gauss = tiles("gauss", 8, [P, HALF], F32)
-        h_planes = tiles("h_planes", 4, [P, PACK, HALF], F32)
-        bias = sb.tile([P, PACK], F32, name="bias")
-        warm = sb.tile([P, 2], F32, name="warm")
-        banks = [ps.tile([P, HALF], F32, name="bank%d" % i) for i in range(8)]
+        g_rows = tiles("g_rows", 2 * PACK, [P, T], F32)
+        gauss = tiles("gauss", PACK, [P, S], F32)
+        h_planes = tiles("h_planes", 2, [P, PACK, S], F32)
+        bias = tile("bias", [P, PACK], F32)
+        banks = [[ps.tile([P, HALF], F32, name="bank%d%d" % (h, t)) for t in range(PACK)] for h in range(2)]
 
         g_view = gT.rearrange("(b p t) c -> b t p c", p=P, t=PACK)
         out_view = out.rearrange("(p t) j -> t p j", t=PACK)
-        turn = []
 
-        def next_grouped():
-            turn.append(0)
-            return grouped[len(turn) % len(grouped)]
-
-        def cast(engine, dst, src):
-            if engine == "scalar":
-                nc.scalar.copy(dst, src)
+        def round_copy(on_scalar, dst, src):
+            if on_scalar:
+                nc.scalar.activation(dst, src, ACT.Copy)
             else:
                 nc.vector.tensor_copy(dst, src)
 
@@ -82,192 +82,174 @@ def tile_list_pair_distance_messages_kernel(
             nc.sync.dma_start(dst[:], src.rearrange("p c i -> p (c i)").bitcast(I32))
 
         def load_scales(dst, src):
-            passes = src.shape[0]
-            for q in range(4):
-                nc.sync.dma_start(dst[32 * q : 32 * q + 4 * passes, :], src[:, 4 * q : 4 * q + 4, :].bitcast(I32))
+            rows = PACK * src.shape[0]
+            for q in range(P // QUADRANT):
+                nc.sync.dma_start(
+                    dst[QUADRANT * q : QUADRANT * q + rows, :], src[:, PACK * q : PACK * (q + 1), :].bitcast(I32)
+                )
 
         def load_weight(dst, w, a, b):
-            rows = w[a * PASS : (a + 1) * PASS, b * PASS : (b + 1) * PASS]
-            nc.sync.dma_start(dst[:], rows.rearrange("(p j) c -> p j c", j=PACK))
+            piece = w[a * PASS : (a + 1) * PASS, b * PASS : (b + 1) * PASS]
+            nc.sync.dma_start(dst[:], piece.rearrange("(p i) c -> p i c", i=PACK))
 
         def load_g(b, t):
             nc.sync.dma_start(g_rows[PACK * b + t][:], g_view[b, t])
 
-        def quantize_weight(src, codes, scales, engines):
-            stage = next_grouped()
-            dst_view = stage[:].rearrange("p (t m j) -> p m j t", t=PACK, j=PACK)
-            src_view = src[:].rearrange("p j (m t) -> p m j t", t=PACK)
-            step = P // len(engines)
-            for i, engine in enumerate(engines):
-                cast(engine, dst_view[:, i * step : (i + 1) * step], src_view[:, i * step : (i + 1) * step])
-            nc.vector.quantize_mx(out=codes.bitcast(FP8X4), scales=scales, in_=stage[:])
+        def entries(lst, j):
+            return lst[:, j.start // PER_COLUMN : j.stop // PER_COLUMN]
 
-        def cols(half):
-            return slice(half * HALF, (half + 1) * HALF)
+        def pick(dst, table, dtype, lst, j):
+            nc.vector.tensor_copy(dst[:, j], table[:].bitcast(dtype).indirect(entries(lst, j)))
 
-        def entries(lst, half):
-            return lst[:, half * LIST_COLS : (half + 1) * LIST_COLS]
+        def round_weight(dst, src, scalar_does):
+            dst = dst.rearrange("p (t m i) -> p m i t", t=PACK, i=PACK)
+            src = src[:].rearrange("p i (m t) -> p m i t", t=PACK)
+            for on_scalar, m in zip(scalar_does, (slice(0, P // 2), slice(P // 2, P))):
+                round_copy(on_scalar, dst[:, m], src[:, m])
 
-        def pick(dst, table, dtype, lst, half):
-            nc.vector.tensor_copy(dst[:, cols(half)], table[:].bitcast(dtype).indirect(entries(lst, half)))
+        def round_h(dst, b, j, scalar_does):
+            dst = dst.rearrange("p (c i t) -> p c t i", i=4, t=PACK)
+            src = h_planes[b][:, :, j].rearrange("p t (c i) -> p c t i", i=4)
+            for on_scalar, c in zip(scalar_does, (slice(0, HALF // 8), slice(HALF // 8, HALF // 4))):
+                round_copy(on_scalar, dst[:, c], src[:, c])
 
-        def gaussian(b, t, half):
-            unit = (PACK * b + t) * HALVES + half
-            bank = banks[unit % 8]
-            r = slice(b * PASS + t * P, b * PASS + (t + 1) * P)
+        def quantize(words, scales, src):
+            nc.vector.quantize_mx(out=words.bitcast(FP8X4), scales=scales, in_=src)
+
+        def square_of_d(plane, b, t, half):
+            bank, j, m = banks[half][t], HALVES[half], slice(t * P, (t + 1) * P)
             for a in range(2):
                 nc.tensor.matmul_mx(
                     bank[:],
-                    lhsT=wa_codes[a][:, r].bitcast(FP8X4),
-                    lhsT_scale=wa_scales[a][:, r],
-                    rhs=pick_words[a][:, cols(half)].bitcast(FP8X4),
-                    rhs_scale=pick_scales[4 * a :, cols(half)],
+                    lhsT=wa_words[b][:, a, m].bitcast(FP8X4),
+                    lhsT_scale=wa_scales[b][:, a, m],
+                    rhs=atom_words[a][:, j].bitcast(FP8X4),
+                    rhs_scale=atom_scales[PACK * a :, j],
                     start=(a == 0),
                     stop=False,
                 )
+            r = b * PASS + t * P
             nc.tensor.matmul_mx(
                 bank[:],
-                lhsT=wb_words[:, 2 * r.start : 2 * r.stop].bitcast(FP4X4),
-                lhsT_scale=wb_scales[:, r],
-                rhs=pick2_words[:, cols(half)].bitcast(FP8X4),
-                rhs_scale=pick2_scales[:, cols(half)],
+                lhsT=wb_words[:, 2 * r : 2 * (r + P)].bitcast(FP4X4),
+                lhsT_scale=wb_scales[:, r : r + P],
+                rhs=partner_words[:, j].bitcast(FP8X4),
+                rhs_scale=partner_scales[:, j],
                 start=False,
                 stop=True,
             )
-            e = gauss[unit % 8]
-            nc.scalar.activation(e[:], bank[:], ACT.Square)
-            nc.scalar.activation(e[:], e[:], ACT.Exp, scale=-1.0)
+            nc.scalar.activation(plane[:, j], bank[:], ACT.Square)
 
-        def weigh(b, t, half):
-            unit = (PACK * b + t) * HALVES + half
-            nc.vector.tensor_tensor(
-                h_planes[HALVES * b + half][:, t, :],
-                g_rows[PACK * b + t][:].indirect(entries(atoms, half)),
-                gauss[unit % 8][:],
-                ALU.mult,
-            )
-
-        def quantize_h(b, half, engines):
-            stage = next_grouped()
-            dst_view = stage[:].rearrange("p (c i t) -> p c t i", i=4, t=PACK)
-            src_view = h_planes[HALVES * b + half][:].rearrange("p t (c i) -> p c t i", i=4)
-            step = (HALF // 4) // len(engines)
-            for i, engine in enumerate(engines):
-                cast(engine, dst_view[:, i * step : (i + 1) * step], src_view[:, i * step : (i + 1) * step])
-            nc.vector.quantize_mx(
-                out=h_codes[b][:, cols(half)].bitcast(FP8X4), scales=h_scales[b][:, cols(half)], in_=stage[:]
-            )
+        def weigh(plane, b, t, j):
+            window = g_rows[PACK * b + t][:].indirect(entries(atoms, j))
+            nc.vector.tensor_tensor(h_planes[b][:, t, j], window, plane[:, j], ALU.mult)
 
         def message_pass(b, half):
             for t in range(PACK):
-                n = slice(t * P, (t + 1) * P)
+                m = slice(t * P, (t + 1) * P)
                 nc.tensor.matmul_mx(
-                    banks[PACK * half + t][:],
-                    lhsT=wm_codes[b][:, n].bitcast(FP8X4),
-                    lhsT_scale=wm_scales[b][:, n],
-                    rhs=h_codes[b][:, cols(half)].bitcast(FP8X4),
-                    rhs_scale=h_scales[b][:, cols(half)],
+                    banks[half][t][:],
+                    lhsT=wm_words[b][:, m].bitcast(FP8X4),
+                    lhsT_scale=wm_scales[b][:, m],
+                    rhs=h_words[b][:, HALVES[half]].bitcast(FP8X4),
+                    rhs_scale=h_scales[b][:, HALVES[half]],
                     start=(b == 0),
                     stop=(b == 1),
                 )
 
         def finish(half):
             for t in range(PACK):
-                staged = gauss[PACK * half + t]
-                bank = banks[PACK * half + t]
-                if half == 0 or t % 2 == 0:
-                    nc.scalar.activation(staged[:], bank[:], ACT.Identity, bias=bias[:, t : t + 1])
+                result = gauss[t][:, HALVES[half]]
+                if t % 2 == 0:
+                    nc.scalar.activation(result, banks[half][t][:], ACT.Identity, bias=bias[:, t : t + 1])
                 else:
-                    nc.vector.tensor_scalar(staged[:], bank[:], bias[:, t : t + 1], None, ALU.add)
-                nc.sync.dma_start(out_view[t][:, cols(half)], staged[:])
+                    nc.vector.tensor_scalar(result, banks[half][t][:], bias[:, t : t + 1], None, ALU.add)
+                nc.sync.dma_start(out_view[t][:, HALVES[half]], result)
 
-        SS = ("scalar", "scalar")
-        VV = ("vector",)
-        SV = ("scalar", "vector")
-        SSSV = ("scalar", "scalar", "scalar", "vector")
-        SVVV = ("scalar", "vector", "vector", "vector")
+        SCALAR, VECTOR, SHARED = (True, True), (False, False), (True, False)
 
-        nc.gpsimd.memset(wb_scales_raw[:], 0)
+        nc.gpsimd.memset(wb_scales_in[:], 0)
         nc.gpsimd.memset(v_scales[:], 0)
         nc.vector.memset(v2_scales[:], 0)
-        nc.vector.memset(warm[:, 0:1], 0.0)
-        nc.scalar.activation(warm[:, 1:2], warm[:, 0:1], ACT.Exp)
 
-        nc.sync.dma_start(wb_words_raw[:], wb4_words[0].bitcast(I32))
-        load_scales(wb_scales_raw, wb4_scales)
+        nc.sync.dma_start(wb_words_in[:], wb4_words[0].bitcast(I32))
+        load_scales(wb_scales_in, wb4_scales)
         nc.sync.dma_start(atoms[:], offs)
         load_words(v_words[0], tab_words[0])
         load_scales(v_scales, tab_scales)
-        load_weight(raw[0], wa, 0, 0)
+        load_weight(weight_in[0], wa, 0, 0)
         nc.sync.dma_start(partners[:], offs2)
-        load_words(v_words[1], tab_words[1])
         load_scales(v2_scales, tab2_scales)
-        load_weight(raw[1], wa, 1, 0)
+        load_words(v_words[1], tab_words[1])
+        load_weight(weight_in[1], wa, 1, 0)
         load_words(v2_words, tab2_words[0])
-        load_weight(raw[2], wa, 0, 1)
-        load_weight(raw[3], wa, 1, 1)
+        load_weight(weight_in[2], wa, 0, 1)
+        load_weight(weight_in[3], wa, 1, 1)
+
         for b in range(2):
+            c = slice(2 * b * PASS, 2 * (b + 1) * PASS)
             nc.vector.tensor_copy(
-                wb_words[:, 2 * b * PASS : 2 * (b + 1) * PASS].rearrange("p (t m e) -> p t m e", t=PACK, e=2),
-                wb_words_raw[:].bitcast(U8)[:, 2 * b * PASS : 2 * (b + 1) * PASS].rearrange(
-                    "p (m t e) -> p t m e", t=PACK, e=2
-                ),
+                wb_words[:, c].rearrange("p (t m e) -> p t m e", t=PACK, e=2),
+                wb_words_in[:].bitcast(U8)[:, c].rearrange("p (m t e) -> p t m e", t=PACK, e=2),
             )
         nc.vector.tensor_copy(
             wb_scales[:].rearrange("p (b t m) -> p b t m", b=2, t=PACK),
-            wb_scales_raw[:].bitcast(U8).rearrange("p (b m t) -> p b t m", b=2, t=PACK),
+            wb_scales_in[:].bitcast(U8).rearrange("p (b m t) -> p b t m", b=2, t=PACK),
+        )
+        round_weight(staged[0], weight_in[0], SHARED)
+        round_weight(staged[1], weight_in[1], SCALAR)
+
+        for b, t in [(b, t) for b in range(2) for t in range(PACK)][:-1]:
+            load_g(b, t)
+        load_weight(weight_in[0], wm, 0, 0)
+        load_weight(weight_in[1], wm, 1, 0)
+        load_g(1, PACK - 1)
+        nc.sync.dma_start(bias[:], bm.rearrange("(p t) -> p t", t=PACK))
+
+        pick(atom_words[0], v_words[0], U32, atoms, WHOLE)
+        pick(atom_scales, v_scales, U8, atoms, WHOLE)
+        pick(partner_scales, v2_scales, U8, partners, WHOLE)
+        quantize(wa_words[0][:, 0, :], wa_scales[0][:, 0, :], staged[0])
+        pick(atom_words[1], v_words[1], U32, atoms, WHOLE)
+        quantize(wa_words[0][:, 1, :], wa_scales[0][:, 1, :], staged[1])
+        for j in HALVES:
+            pick(partner_words, v2_words, U32, partners, j)
+        round_weight(staged[2], weight_in[2], VECTOR)
+        round_weight(staged[3], weight_in[3], VECTOR)
+        quantize(
+            wa_words[1][:].rearrange("p a c -> p (a c)"),
+            wa_scales[1][:].rearrange("p a c -> p (a c)"),
+            staged_pairs[1][:].rearrange("p a c -> p (a c)"),
         )
 
-        pick(pick_words[0], v_words[0], U32, atoms, 0)
-        pick(pick_scales, v_scales, U8, atoms, 0)
-        quantize_weight(raw[0], wa_codes[0][:, 0:PASS], wa_scales[0][:, 0:PASS], SS)
-        pick(pick_words[1], v_words[1], U32, atoms, 0)
-        pick(pick2_scales, v2_scales, U8, partners, 0)
-        quantize_weight(raw[1], wa_codes[1][:, 0:PASS], wa_scales[1][:, 0:PASS], SS)
-        pick(pick2_words, v2_words, U32, partners, 0)
-        load_weight(raw[0], wm, 0, 0)
-        load_g(0, 0)
-        load_g(0, 1)
-        load_g(0, 2)
-        load_g(0, 3)
-        nc.sync.dma_start(bias[:], bm.rearrange("(p t) -> p t", t=PACK))
-        load_weight(raw[1], wm, 1, 0)
-        load_g(1, 0)
-        load_g(1, 1)
-        load_g(1, 2)
-        load_g(1, 3)
-
+        late = [tile("v_words%d" % i, [P, 2, S], F32) for i in range(2)]
+        planes = [[gauss[t][:] for t in range(PACK)], [late[t // 2][:, t % 2, :] for t in range(PACK)]]
+        for b in range(2):
+            for t0 in range(0, PACK, 2):
+                for half in range(2):
+                    for t in (t0, t0 + 1):
+                        square_of_d(planes[b][t], b, t, half)
+                for t in (t0, t0 + 1):
+                    nc.scalar.activation(planes[b][t], planes[b][t], ACT.Exp, scale=-1.0)
         for t in range(PACK):
-            gaussian(0, t, 0)
-        pick(pick_words[0], v_words[0], U32, atoms, 1)
-        pick(pick_scales, v_scales, U8, atoms, 1)
-        pick(pick_words[1], v_words[1], U32, atoms, 1)
-        pick(pick2_scales, v2_scales, U8, partners, 1)
-        pick(pick2_words, v2_words, U32, partners, 1)
-        for a in range(2):
-            quantize_weight(raw[2 + a], wa_codes[a][:, PASS:H], wa_scales[a][:, PASS:H], SS)
-        for t in range(PACK):
-            gaussian(0, t, 1)
-        for t in range(PACK):
-            for half in range(HALVES):
-                weigh(0, t, half)
-            for half in range(HALVES):
-                gaussian(1, t, half)
-            if t == 0:
-                quantize_weight(raw[0], wm_codes[0][:], wm_scales[0][:], SS)
+            for j in (WHOLE,):
+                weigh(planes[0][t], 0, t, j)
+        round_h(staged[0], 0, HALVES[0], VECTOR)
+        round_weight(staged[2], weight_in[0], SCALAR)
+        round_h(staged[1], 0, HALVES[1], SHARED)
+        round_weight(staged[3], weight_in[1], SCALAR)
+        for i in range(2):
+            quantize(h_words[0][:, HALVES[i]], h_scales[0][:, HALVES[i]], staged[i])
+            quantize(wm_words[i][:], wm_scales[i][:], staged[2 + i])
+        for half in range(2):
+            message_pass(0, half)
         for t in range(PACK - 1):
-            if t < 2:
-                quantize_h(0, t, (SV, SV)[t])
-            for half in range(HALVES):
-                weigh(1, t, half)
-        quantize_weight(raw[1], wm_codes[1][:], wm_scales[1][:], SS)
-        message_pass(0, 0)
-        message_pass(0, 1)
-        weigh(1, 3, 0)
-        quantize_h(1, 0, SV)
-        message_pass(1, 0)
-        weigh(1, 3, 1)
-        quantize_h(1, 1, SV)
-        finish(0)
-        message_pass(1, 1)
-        finish(1)
+            for j in (WHOLE,):
+                weigh(planes[1][t], 1, t, j)
+        for half in range(2):
+            weigh(planes[1][PACK - 1], 1, PACK - 1, HALVES[half])
+            round_h(staged[half], 1, HALVES[half], SHARED)
+            quantize(h_words[1][:, HALVES[half]], h_scales[1][:, HALVES[half]], staged[half])
+            message_pass(1, half)
+        for half in range(2):
+            finish(half)

@@ -21,9 +21,13 @@ PACK = 4
 PASS = P * PACK
 HALF = 512
 QUADRANT = 32
+SCALE_ROWS = 4
+I32_BYTES = 4
 PER_COLUMN = 16
 HALVES = (slice(0, HALF), slice(HALF, S))
 WHOLE = slice(0, S)
+QUARTER = HALF // 2
+RUN = 4
 
 
 def tile_list_pair_distance_messages_kernel(
@@ -43,11 +47,11 @@ def tile_list_pair_distance_messages_kernel(
         atoms = sb.tile([P, S // PER_COLUMN], U16, name="atoms")
         partners = sb.tile([P, S // PER_COLUMN], U16, name="partners")
         v_words = tiles("v_words", 2, [P, T], I32)
-        v_scales = tile("v_scales", [P, T // 4], I32)
+        v_scales = tile("v_scales", [P, T // I32_BYTES], I32)
         v2_words = tile("v2_words", [P, T], I32)
-        v2_scales = tile("v2_scales", [P, T // 4], I32)
-        wb_words_in = tile("wb_words_in", [P, H // 2], I32)
-        wb_scales_in = tile("wb_scales_in", [P, H // 4], I32)
+        v2_scales = tile("v2_scales", [P, T // I32_BYTES], I32)
+        wb_words_in = tile("wb_words_in", [P, 2 * H // I32_BYTES], I32)
+        wb_scales_in = tile("wb_scales_in", [P, H // I32_BYTES], I32)
         wb_words = tile("wb_words", [P, 2 * H], U8)
         wb_scales = tile("wb_scales", [P, H], U8)
         atom_words = tiles("atom_words", 2, [P, S], U32)
@@ -67,7 +71,7 @@ def tile_list_pair_distance_messages_kernel(
         gauss = tiles("gauss", PACK, [P, S], F32)
         h_planes = tiles("h_planes", 2, [P, PACK, S], F32)
         bias = tile("bias", [P, PACK], F32)
-        banks = [[ps.tile([P, HALF], F32, name="bank%d%d" % (h, t)) for t in range(PACK)] for h in range(2)]
+        banks = [[ps.tile([P, HALF], F32, name="bank%d%d" % (half, t)) for t in range(PACK)] for half in range(2)]
 
         g_view = gT.rearrange("(b p t) c -> b t p c", p=P, t=PACK)
         out_view = out.rearrange("(p t) j -> t p j", t=PACK)
@@ -82,11 +86,10 @@ def tile_list_pair_distance_messages_kernel(
             nc.sync.dma_start(dst[:], src.rearrange("p c i -> p (c i)").bitcast(I32))
 
         def load_scales(dst, src):
-            rows = PACK * src.shape[0]
-            for q in range(P // QUADRANT):
-                nc.sync.dma_start(
-                    dst[QUADRANT * q : QUADRANT * q + rows, :], src[:, PACK * q : PACK * (q + 1), :].bitcast(I32)
-                )
+            rows = SCALE_ROWS * src.shape[0]
+            for quad in range(P // QUADRANT):
+                blocks = src[:, SCALE_ROWS * quad : SCALE_ROWS * (quad + 1), :]
+                nc.sync.dma_start(dst[QUADRANT * quad : QUADRANT * quad + rows, :], blocks.bitcast(I32))
 
         def load_weight(dst, w, a, b):
             piece = w[a * PASS : (a + 1) * PASS, b * PASS : (b + 1) * PASS]
@@ -108,10 +111,11 @@ def tile_list_pair_distance_messages_kernel(
                 round_copy(on_scalar, dst[:, m], src[:, m])
 
         def round_h(dst, b, j, scalar_does):
-            dst = dst.rearrange("p (c i t) -> p c t i", i=4, t=PACK)
-            src = h_planes[b][:, :, j].rearrange("p t (c i) -> p c t i", i=4)
-            for on_scalar, c in zip(scalar_does, (slice(0, HALF // 8), slice(HALF // 8, HALF // 4))):
-                round_copy(on_scalar, dst[:, c], src[:, c])
+            runs = HALF // RUN
+            dst = dst.rearrange("p (run e t) -> p run t e", e=RUN, t=PACK)
+            src = h_planes[b][:, :, j].rearrange("p t (run e) -> p run t e", e=RUN)
+            for on_scalar, part in zip(scalar_does, (slice(0, runs // 2), slice(runs // 2, runs))):
+                round_copy(on_scalar, dst[:, part], src[:, part])
 
         def quantize(words, scales, src):
             nc.vector.quantize_mx(out=words.bitcast(FP8X4), scales=scales, in_=src)
@@ -124,7 +128,7 @@ def tile_list_pair_distance_messages_kernel(
                     lhsT=wa_words[b][:, a, m].bitcast(FP8X4),
                     lhsT_scale=wa_scales[b][:, a, m],
                     rhs=atom_words[a][:, j].bitcast(FP8X4),
-                    rhs_scale=atom_scales[PACK * a :, j],
+                    rhs_scale=atom_scales[SCALE_ROWS * a :, j],
                     start=(a == 0),
                     stop=False,
                 )
@@ -186,17 +190,15 @@ def tile_list_pair_distance_messages_kernel(
         load_weight(weight_in[2], wa, 0, 1)
         load_weight(weight_in[3], wa, 1, 1)
 
-        for b in range(2):
-            c = slice(2 * b * PASS, 2 * (b + 1) * PASS)
-            nc.vector.tensor_copy(
-                wb_words[:, c].rearrange("p (t m e) -> p t m e", t=PACK, e=2),
-                wb_words_in[:].bitcast(U8)[:, c].rearrange("p (m t e) -> p t m e", t=PACK, e=2),
-            )
+        nc.vector.tensor_copy(
+            wb_words[:].bitcast(U16).rearrange("p (b t m) -> p b t m", b=2, t=PACK),
+            wb_words_in[:].bitcast(U16).rearrange("p (b m t) -> p b t m", b=2, t=PACK),
+        )
         nc.vector.tensor_copy(
             wb_scales[:].rearrange("p (b t m) -> p b t m", b=2, t=PACK),
             wb_scales_in[:].bitcast(U8).rearrange("p (b m t) -> p b t m", b=2, t=PACK),
         )
-        round_weight(staged[0], weight_in[0], SHARED)
+        round_weight(staged[0], weight_in[0], SCALAR)
         round_weight(staged[1], weight_in[1], SCALAR)
 
         for b, t in [(b, t) for b in range(2) for t in range(PACK)][:-1]:
@@ -222,8 +224,8 @@ def tile_list_pair_distance_messages_kernel(
             staged_pairs[1][:].rearrange("p a c -> p (a c)"),
         )
 
-        late = [tile("v_words%d" % i, [P, 2, S], F32) for i in range(2)]
-        planes = [[gauss[t][:] for t in range(PACK)], [late[t // 2][:, t % 2, :] for t in range(PACK)]]
+        gauss_late = [tile("v_words%d" % i, [P, 2, S], F32) for i in range(2)]
+        planes = [[gauss[t][:] for t in range(PACK)], [gauss_late[t // 2][:, t % 2, :] for t in range(PACK)]]
         for b in range(2):
             for t0 in range(0, PACK, 2):
                 for half in range(2):
@@ -231,9 +233,9 @@ def tile_list_pair_distance_messages_kernel(
                         square_of_d(planes[b][t], b, t, half)
                 for t in (t0, t0 + 1):
                     nc.scalar.activation(planes[b][t], planes[b][t], ACT.Exp, scale=-1.0)
+
         for t in range(PACK):
-            for j in (WHOLE,):
-                weigh(planes[0][t], 0, t, j)
+            weigh(planes[0][t], 0, t, WHOLE)
         round_h(staged[0], 0, HALVES[0], VECTOR)
         round_weight(staged[2], weight_in[0], SCALAR)
         round_h(staged[1], 0, HALVES[1], SHARED)
@@ -243,11 +245,12 @@ def tile_list_pair_distance_messages_kernel(
             quantize(wm_words[i][:], wm_scales[i][:], staged[2 + i])
         for half in range(2):
             message_pass(0, half)
+
         for t in range(PACK - 1):
-            for j in (WHOLE,):
-                weigh(planes[1][t], 1, t, j)
+            weigh(planes[1][t], 1, t, WHOLE)
         for half in range(2):
-            weigh(planes[1][PACK - 1], 1, PACK - 1, HALVES[half])
+            for j0 in range(HALVES[half].start, HALVES[half].stop, QUARTER):
+                weigh(planes[1][PACK - 1], 1, PACK - 1, slice(j0, j0 + QUARTER))
             round_h(staged[half], 1, HALVES[half], SHARED)
             quantize(h_words[1][:, HALVES[half]], h_scales[1][:, HALVES[half]], staged[half])
             message_pass(1, half)

@@ -27,7 +27,7 @@ PER_COLUMN = 16
 HALVES = (slice(0, HALF), slice(HALF, S))
 WHOLE = slice(0, S)
 QUARTER = HALF // 2
-RUN = 4
+RUN = 2
 
 
 def tile_list_pair_distance_messages_kernel(
@@ -58,23 +58,15 @@ def tile_list_pair_distance_messages_kernel(
         atom_scales = tile("atom_scales", [P, S], U8)
         partner_words = tile("partner_words", [P, S], U32)
         partner_scales = tile("partner_scales", [P, S], U8)
-        weight_in = tiles("weight_in", 4, [P, PACK, PASS], F32)
-        staged_pairs = tiles("staged", 2, [P, 2, PACK * PASS], BF16)
-        staged = [staged_pairs[i // 2][:, i % 2, :] for i in range(4)]
-        wa_words = tiles("wa_words", 2, [P, 2, PASS], U32)
-        wa_scales = tiles("wa_scales", 2, [P, 2, PASS], U8)
-        wm_words = tiles("wm_words", 2, [P, N], U32)
+        wa_words = [tiles("wa_words%d" % b, 2, [P, PASS], U32) for b in range(2)]
+        wa_scales = [tiles("wa_scales%d" % b, 2, [P, PASS], U8) for b in range(2)]
         wm_scales = tiles("wm_scales", 2, [P, N], U8)
-        h_words = tiles("h_words", 2, [P, S], U32)
-        h_scales = tiles("h_scales", 2, [P, S], U8)
         g_rows = tiles("g_rows", 2 * PACK, [P, T], F32)
-        gauss = tiles("gauss", PACK, [P, S], F32)
         h_planes = tiles("h_planes", 2, [P, PACK, S], F32)
         bias = tile("bias", [P, PACK], F32)
-        banks = [[ps.tile([P, HALF], F32, name="bank%d%d" % (half, t)) for t in range(PACK)] for half in range(2)]
 
         g_view = gT.rearrange("(b p t) c -> b t p c", p=P, t=PACK)
-        out_view = out.rearrange("(p t) j -> t p j", t=PACK)
+        out_view = out.rearrange("(t p) j -> p t j", p=P)
 
         def round_copy(on_scalar, dst, src):
             if on_scalar:
@@ -87,13 +79,19 @@ def tile_list_pair_distance_messages_kernel(
 
         def load_scales(dst, src):
             rows = SCALE_ROWS * src.shape[0]
+            if rows == SCALE_ROWS:
+                for r in range(SCALE_ROWS):
+                    nc.sync.dma_start(dst[r:P:QUADRANT, :], src[0, r::SCALE_ROWS, :].bitcast(I32))
+                return
             for quad in range(P // QUADRANT):
                 blocks = src[:, SCALE_ROWS * quad : SCALE_ROWS * (quad + 1), :]
                 nc.sync.dma_start(dst[QUADRANT * quad : QUADRANT * quad + rows, :], blocks.bitcast(I32))
 
-        def load_weight(dst, w, a, b):
+        def load_weight(slot, w, a, b):
+            dst = tile("weight_in%d" % slot, [P, PACK, PASS], F32)
             piece = w[a * PASS : (a + 1) * PASS, b * PASS : (b + 1) * PASS]
             nc.sync.dma_start(dst[:], piece.rearrange("(p i) c -> p i c", i=PACK))
+            return dst
 
         def load_g(b, t):
             nc.sync.dma_start(g_rows[PACK * b + t][:], g_view[b, t])
@@ -104,29 +102,40 @@ def tile_list_pair_distance_messages_kernel(
         def pick(dst, table, dtype, lst, j):
             nc.vector.tensor_copy(dst[:, j], table[:].bitcast(dtype).indirect(entries(lst, j)))
 
-        def round_weight(dst, src, scalar_does):
-            dst = dst.rearrange("p (t m i) -> p m i t", t=PACK, i=PACK)
+        def round_weight(slot, src, scalar_does):
+            staged = tile("staged%d" % slot, [P, PACK * PASS], BF16)
+            dst = staged[:].rearrange("p (t m i) -> p m i t", t=PACK, i=PACK)
             src = src[:].rearrange("p i (m t) -> p m i t", t=PACK)
-            for on_scalar, m in zip(scalar_does, (slice(0, P // 2), slice(P // 2, P))):
-                round_copy(on_scalar, dst[:, m], src[:, m])
+            for on_scalar, t in zip(scalar_does, (slice(0, 2), slice(2, PACK))):
+                round_copy(on_scalar, dst[:, :, :, t], src[:, :, :, t])
+            return staged
 
-        def round_h(dst, b, j, scalar_does):
-            runs = HALF // RUN
-            dst = dst.rearrange("p (run e t) -> p run t e", e=RUN, t=PACK)
-            src = h_planes[b][:, :, j].rearrange("p t (run e) -> p run t e", e=RUN)
-            for on_scalar, part in zip(scalar_does, (slice(0, runs // 2), slice(runs // 2, runs))):
-                round_copy(on_scalar, dst[:, part], src[:, part])
+        def quantize_weight(words, scales, staged):
+            for part in range(2):
+                c = slice(part * PASS // 2, (part + 1) * PASS // 2)
+                quantize(words[:, c], scales[:, c], staged[:, PACK * c.start : PACK * c.stop])
+
+        def round_rows(slot, src, scalar_does):
+            columns = src.shape[2]
+            staged = tile("staged%d" % slot, [P, PACK * columns], BF16)
+            dst = staged[:].rearrange("p (run e t) -> p run t e", e=RUN, t=PACK)
+            src = src.rearrange("p t (run e) -> p run t e", e=RUN)
+            runs = columns // RUN // len(scalar_does)
+            for part, on_scalar in enumerate(scalar_does):
+                round_copy(on_scalar, dst[:, part * runs : (part + 1) * runs], src[:, part * runs : (part + 1) * runs])
+            return staged
 
         def quantize(words, scales, src):
             nc.vector.quantize_mx(out=words.bitcast(FP8X4), scales=scales, in_=src)
 
-        def square_of_d(plane, b, t, half):
-            bank, j, m = banks[half][t], HALVES[half], slice(t * P, (t + 1) * P)
+        def square_of_d(dst, b, t, half):
+            bank = ps.tile([P, HALF], F32, name="bank%d" % (2 * (t % 2) + half))
+            j, m = HALVES[half], slice(t * P, (t + 1) * P)
             for a in range(2):
                 nc.tensor.matmul_mx(
                     bank[:],
-                    lhsT=wa_words[b][:, a, m].bitcast(FP8X4),
-                    lhsT_scale=wa_scales[b][:, a, m],
+                    lhsT=wa_words[b][a][:, m].bitcast(FP8X4),
+                    lhsT_scale=wa_scales[b][a][:, m],
                     rhs=atom_words[a][:, j].bitcast(FP8X4),
                     rhs_scale=atom_scales[SCALE_ROWS * a :, j],
                     start=(a == 0),
@@ -142,54 +151,75 @@ def tile_list_pair_distance_messages_kernel(
                 start=False,
                 stop=True,
             )
-            nc.scalar.activation(plane[:, j], bank[:], ACT.Square)
+            nc.scalar.activation(dst, bank[:], ACT.Square)
 
-        def weigh(plane, b, t, j):
+        def gaussian_half(dst, b, t, half):
+            square = tile("square%d" % half, [P, HALF], F32)
+            square_of_d(square[:], b, t, half)
+            nc.scalar.activation(dst, square[:], ACT.Exp, scale=-1.0)
+
+        def gaussian(name, b, t):
+            plane = tile(name, [P, S], F32)
+            for half in range(2):
+                gaussian_half(plane[:, HALVES[half]], b, t, half)
+            return plane
+
+        def weigh(factor, b, t, j):
             window = g_rows[PACK * b + t][:].indirect(entries(atoms, j))
-            nc.vector.tensor_tensor(h_planes[b][:, t, j], window, plane[:, j], ALU.mult)
+            nc.vector.tensor_tensor(h_planes[b][:, t, j], window, factor, ALU.mult)
 
-        def message_pass(b, half):
+        def message_pass(b, sums, w_words, words, scales):
             for t in range(PACK):
                 m = slice(t * P, (t + 1) * P)
                 nc.tensor.matmul_mx(
-                    banks[half][t][:],
-                    lhsT=wm_words[b][:, m].bitcast(FP8X4),
+                    sums[t // 2][:, t % 2, :],
+                    lhsT=w_words[:, m].bitcast(FP8X4),
                     lhsT_scale=wm_scales[b][:, m],
-                    rhs=h_words[b][:, HALVES[half]].bitcast(FP8X4),
-                    rhs_scale=h_scales[b][:, HALVES[half]],
-                    start=(b == 0),
-                    stop=(b == 1),
+                    rhs=words.bitcast(FP8X4),
+                    rhs_scale=scales,
+                    start=(b == 0 and t % 2 == 0),
+                    stop=(b == 1 and t % 2 == 1),
                 )
 
-        def finish(half):
-            for t in range(PACK):
-                result = gauss[t][:, HALVES[half]]
-                if t % 2 == 0:
-                    nc.scalar.activation(result, banks[half][t][:], ACT.Identity, bias=bias[:, t : t + 1])
+        def finish(name, bank, pair, j, on_scalar):
+            result = tile(name, [P, 2, QUARTER], F32)
+            for i in range(2):
+                column = bias[:, 2 * pair + i : 2 * pair + i + 1]
+                if on_scalar:
+                    nc.scalar.activation(result[:, i, :], bank[:, i, :], ACT.Identity, bias=column)
                 else:
-                    nc.vector.tensor_scalar(result, banks[half][t][:], bias[:, t : t + 1], None, ALU.add)
-                nc.sync.dma_start(out_view[t][:, HALVES[half]], result)
+                    nc.vector.tensor_scalar(result[:, i, :], bank[:, i, :], column, None, ALU.add)
+            nc.sync.dma_start(out_view[:, 2 * pair : 2 * pair + 2, j], result[:])
 
         SCALAR, VECTOR, SHARED = (True, True), (False, False), (True, False)
 
+        nc.vector.memset(v_scales[:], 0)
+        nc.gpsimd.memset(v2_scales[:], 0)
         nc.gpsimd.memset(wb_scales_in[:], 0)
-        nc.gpsimd.memset(v_scales[:], 0)
-        nc.vector.memset(v2_scales[:], 0)
 
-        nc.sync.dma_start(wb_words_in[:], wb4_words[0].bitcast(I32))
-        load_scales(wb_scales_in, wb4_scales)
         nc.sync.dma_start(atoms[:], offs)
-        load_words(v_words[0], tab_words[0])
+        nc.sync.dma_start(wb_words_in[:], wb4_words[0].bitcast(I32))
         load_scales(v_scales, tab_scales)
-        load_weight(weight_in[0], wa, 0, 0)
+        load_words(v_words[0], tab_words[0])
         nc.sync.dma_start(partners[:], offs2)
         load_scales(v2_scales, tab2_scales)
+        wa00 = load_weight(0, wa, 0, 0)
         load_words(v_words[1], tab_words[1])
-        load_weight(weight_in[1], wa, 1, 0)
+        load_scales(wb_scales_in, wb4_scales)
+        with nc.allow_non_contiguous_dma(reason="one bias value for each partition and output tile"):
+            nc.sync.dma_start(bias[:], bm.rearrange("(t p) -> p t", p=P))
+        wa10 = load_weight(1, wa, 1, 0)
         load_words(v2_words, tab2_words[0])
-        load_weight(weight_in[2], wa, 0, 1)
-        load_weight(weight_in[3], wa, 1, 1)
+        wa01 = load_weight(2, wa, 0, 1)
+        load_g(0, 0)
+        wa11 = load_weight(3, wa, 1, 1)
 
+        pick(atom_scales, v_scales, U8, atoms, WHOLE)
+        pick(atom_words[0], v_words[0], U32, atoms, WHOLE)
+        staged = round_weight(0, wa00, SCALAR)
+        pick(partner_scales, v2_scales, U8, partners, WHOLE)
+        quantize_weight(wa_words[0][0], wa_scales[0][0], staged)
+        pick(atom_words[1], v_words[1], U32, atoms, WHOLE)
         nc.vector.tensor_copy(
             wb_words[:].bitcast(U16).rearrange("p (b t m) -> p b t m", b=2, t=PACK),
             wb_words_in[:].bitcast(U16).rearrange("p (b m t) -> p b t m", b=2, t=PACK),
@@ -198,61 +228,62 @@ def tile_list_pair_distance_messages_kernel(
             wb_scales[:].rearrange("p (b t m) -> p b t m", b=2, t=PACK),
             wb_scales_in[:].bitcast(U8).rearrange("p (b m t) -> p b t m", b=2, t=PACK),
         )
-        round_weight(staged[0], weight_in[0], SCALAR)
-        round_weight(staged[1], weight_in[1], SCALAR)
-
-        for b, t in [(b, t) for b in range(2) for t in range(PACK)][:-1]:
-            load_g(b, t)
-        load_weight(weight_in[0], wm, 0, 0)
-        load_weight(weight_in[1], wm, 1, 0)
-        load_g(1, PACK - 1)
-        nc.sync.dma_start(bias[:], bm.rearrange("(p t) -> p t", t=PACK))
-
-        pick(atom_words[0], v_words[0], U32, atoms, WHOLE)
-        pick(atom_scales, v_scales, U8, atoms, WHOLE)
-        pick(partner_scales, v2_scales, U8, partners, WHOLE)
-        quantize(wa_words[0][:, 0, :], wa_scales[0][:, 0, :], staged[0])
-        pick(atom_words[1], v_words[1], U32, atoms, WHOLE)
-        quantize(wa_words[0][:, 1, :], wa_scales[0][:, 1, :], staged[1])
+        quantize_weight(wa_words[0][1], wa_scales[0][1], round_weight(1, wa10, SHARED))
         for j in HALVES:
             pick(partner_words, v2_words, U32, partners, j)
-        round_weight(staged[2], weight_in[2], VECTOR)
-        round_weight(staged[3], weight_in[3], VECTOR)
-        quantize(
-            wa_words[1][:].rearrange("p a c -> p (a c)"),
-            wa_scales[1][:].rearrange("p a c -> p (a c)"),
-            staged_pairs[1][:].rearrange("p a c -> p (a c)"),
-        )
 
-        gauss_late = [tile("v_words%d" % i, [P, 2, S], F32) for i in range(2)]
-        planes = [[gauss[t][:] for t in range(PACK)], [gauss_late[t // 2][:, t % 2, :] for t in range(PACK)]]
-        for b in range(2):
-            for t0 in range(0, PACK, 2):
-                for half in range(2):
-                    for t in (t0, t0 + 1):
-                        square_of_d(planes[b][t], b, t, half)
-                for t in (t0, t0 + 1):
-                    nc.scalar.activation(planes[b][t], planes[b][t], ACT.Exp, scale=-1.0)
+        for t in range(1, PACK):
+            load_g(0, t)
+        load_g(1, 0)
+        wm0 = load_weight(0, wm, 0, 0)
+        load_g(1, 1)
+        load_g(1, 2)
+        wm1 = load_weight(1, wm, 1, 0)
+        load_g(1, 3)
 
-        for t in range(PACK):
-            weigh(planes[0][t], 0, t, WHOLE)
-        round_h(staged[0], 0, HALVES[0], VECTOR)
-        round_weight(staged[2], weight_in[0], SCALAR)
-        round_h(staged[1], 0, HALVES[1], SHARED)
-        round_weight(staged[3], weight_in[1], SCALAR)
-        for i in range(2):
-            quantize(h_words[0][:, HALVES[i]], h_scales[0][:, HALVES[i]], staged[i])
-            quantize(wm_words[i][:], wm_scales[i][:], staged[2 + i])
-        for half in range(2):
-            message_pass(0, half)
+        quantize_weight(wa_words[1][0], wa_scales[1][0], round_weight(2, wa01, VECTOR))
+        first = gaussian("gauss0", 0, 0)
+        for j in HALVES:
+            weigh(first[:, j], 0, 0, j)
+        quantize_weight(wa_words[1][1], wa_scales[1][1], round_weight(3, wa11, VECTOR))
+        for t in range(1, PACK):
+            weigh(gaussian("gauss%d" % t, 0, t)[:], 0, t, WHOLE)
 
-        for t in range(PACK - 1):
-            weigh(planes[1][t], 1, t, WHOLE)
+        late = [gaussian(name, 1, t) for t, name in enumerate(("v_words0", "v_words1", "v2_words"))]
+        last = [tile("gauss%d" % half, [P, HALF], F32) for half in range(2)]
         for half in range(2):
-            for j0 in range(HALVES[half].start, HALVES[half].stop, QUARTER):
-                weigh(planes[1][PACK - 1], 1, PACK - 1, slice(j0, j0 + QUARTER))
-            round_h(staged[half], 1, HALVES[half], SHARED)
-            quantize(h_words[1][:, HALVES[half]], h_scales[1][:, HALVES[half]], staged[half])
-            message_pass(1, half)
-        for half in range(2):
-            finish(half)
+            gaussian_half(last[half][:], 1, PACK - 1, half)
+        h0_staged = [round_rows(1 + half, h_planes[0][:, :, HALVES[half]], (SCALAR, SHARED)[half]) for half in range(2)]
+
+        sums = [
+            [ps.tile([P, 2, QUARTER], F32, name="bank%d" % ((4 + 2 * q + pair) % 8)) for pair in range(2)]
+            for q in range(4)
+        ]
+        weigh(late[0][:], 1, 0, WHOLE)
+        wm_words0 = tile("wm_words0", [P, N], U32)
+        quantize_weight(wm_words0, wm_scales[0], round_rows(0, wm0[:], VECTOR))
+        for t in (1, 2):
+            weigh(late[t][:], 1, t, WHOLE)
+        for half, name in enumerate(("v2_words", "g_rows6")):
+            words = tile(name, [P, HALF], U32)
+            scales = tile("h0_scales%d" % half, [P, HALF], U8)
+            quantize(words[:], scales[:], h0_staged[half][:])
+            for i in range(2):
+                c = slice(i * QUARTER, (i + 1) * QUARTER)
+                message_pass(0, sums[2 * half + i], wm_words0, words[:, c], scales[:, c])
+        wm1_staged = round_rows(3, wm1[:], SCALAR)
+
+        quarters = [slice(q * QUARTER, (q + 1) * QUARTER) for q in range(4)]
+        for q, j in enumerate(quarters):
+            weigh(last[q // 2][:, quarters[q % 2]], 1, PACK - 1, j)
+            if q == 1:
+                wm_words1 = tile("gauss0", [P, N], U32)
+                quantize(wm_words1[:], wm_scales[1][:], wm1_staged[:])
+        for q, j in enumerate(quarters):
+            words = tile("h1_words%d" % q, [P, QUARTER], U32)
+            scales = tile("h1_scales%d" % q, [P, QUARTER], U8)
+            quantize(words[:], scales[:], round_rows(q % 2, h_planes[1][:, :, j], (q < 2,))[:])
+            message_pass(1, sums[q], wm_words1, words[:], scales[:])
+        for q, j in enumerate(quarters):
+            for pair in range(2):
+                finish("g_rows%d" % (2 * q + pair), sums[q][pair], pair, j, q < 2 or pair == 0)

@@ -128,13 +128,18 @@ def tile_list_pair_distance_messages_kernel(
         def quantize(words, scales, src):
             nc.vector.quantize_mx(out=words.bitcast(FP8X4), scales=scales, in_=src)
 
+        def wa_columns(b, a, t):
+            if (b, a) == (0, 1) and t >= 2:
+                return late_words[:, (t - 2) * P : (t - 1) * P]
+            return wa_words[b][a][:, t * P : (t + 1) * P]
+
         def square_of_d(dst, b, t, half):
             bank = ps.tile([P, HALF], F32, name="bank%d" % (2 * (t % 2) + half))
             j, m = HALVES[half], slice(t * P, (t + 1) * P)
             for a in range(2):
                 nc.tensor.matmul_mx(
                     bank[:],
-                    lhsT=wa_words[b][a][:, m].bitcast(FP8X4),
+                    lhsT=wa_columns(b, a, t).bitcast(FP8X4),
                     lhsT_scale=wa_scales[b][a][:, m],
                     rhs=atom_words[a][:, j].bitcast(FP8X4),
                     rhs_scale=atom_scales[SCALE_ROWS * a :, j],
@@ -154,7 +159,7 @@ def tile_list_pair_distance_messages_kernel(
             nc.scalar.activation(dst, bank[:], ACT.Square)
 
         def gaussian_half(dst, b, t, half):
-            square = tile("square%d" % half, [P, HALF], F32)
+            square = tile("square%d" % ((2 * (PACK * b + t) + half) % 3), [P, HALF], F32)
             square_of_d(square[:], b, t, half)
             nc.scalar.activation(dst, square[:], ACT.Exp, scale=-1.0)
 
@@ -206,8 +211,6 @@ def tile_list_pair_distance_messages_kernel(
         wa00 = load_weight(0, wa, 0, 0)
         load_words(v_words[1], tab_words[1])
         load_scales(wb_scales_in, wb4_scales)
-        with nc.allow_non_contiguous_dma(reason="one bias value for each partition and output tile"):
-            nc.sync.dma_start(bias[:], bm.rearrange("(t p) -> p t", p=P))
         wa10 = load_weight(1, wa, 1, 0)
         load_words(v2_words, tab2_words[0])
         wa01 = load_weight(2, wa, 0, 1)
@@ -228,9 +231,13 @@ def tile_list_pair_distance_messages_kernel(
             wb_scales[:].rearrange("p (b t m) -> p b t m", b=2, t=PACK),
             wb_scales_in[:].bitcast(U8).rearrange("p (b m t) -> p b t m", b=2, t=PACK),
         )
-        quantize_weight(wa_words[0][1], wa_scales[0][1], round_weight(1, wa10, SHARED))
+        staged = round_weight(1, wa10, SCALAR)
+        half_pass = PASS // 2
+        quantize(wa_words[0][1][:, 0:half_pass], wa_scales[0][1][:, 0:half_pass], staged[:, 0 : PACK * half_pass])
         for j in HALVES:
             pick(partner_words, v2_words, U32, partners, j)
+        late_words = tile("v2_words", [P, half_pass], U32)
+        quantize(late_words[:], wa_scales[0][1][:, half_pass:], staged[:, PACK * half_pass :])
 
         for t in range(1, PACK):
             load_g(0, t)
@@ -240,6 +247,8 @@ def tile_list_pair_distance_messages_kernel(
         load_g(1, 2)
         wm1 = load_weight(1, wm, 1, 0)
         load_g(1, 3)
+        with nc.allow_non_contiguous_dma(reason="one bias value for each partition and output tile"):
+            nc.sync.dma_start(bias[:], bm.rearrange("(t p) -> p t", p=P))
 
         quantize_weight(wa_words[1][0], wa_scales[1][0], round_weight(2, wa01, VECTOR))
         first = gaussian("gauss0", 0, 0)
@@ -253,7 +262,7 @@ def tile_list_pair_distance_messages_kernel(
         last = [tile("gauss%d" % half, [P, HALF], F32) for half in range(2)]
         for half in range(2):
             gaussian_half(last[half][:], 1, PACK - 1, half)
-        h0_staged = [round_rows(1 + half, h_planes[0][:, :, HALVES[half]], (SCALAR, SHARED)[half]) for half in range(2)]
+        h0_staged = [round_rows(1 + half, h_planes[0][:, :, HALVES[half]], SCALAR) for half in range(2)]
 
         sums = [
             [ps.tile([P, 2, QUARTER], F32, name="bank%d" % ((4 + 2 * q + pair) % 8)) for pair in range(2)]
@@ -271,7 +280,7 @@ def tile_list_pair_distance_messages_kernel(
             for i in range(2):
                 c = slice(i * QUARTER, (i + 1) * QUARTER)
                 message_pass(0, sums[2 * half + i], wm_words0, words[:, c], scales[:, c])
-        wm1_staged = round_rows(3, wm1[:], SCALAR)
+        wm1_staged = round_rows(3, wm1[:], SHARED)
 
         quarters = [slice(q * QUARTER, (q + 1) * QUARTER) for q in range(4)]
         for q, j in enumerate(quarters):

@@ -158,15 +158,18 @@ def tile_list_pair_distance_messages_kernel(
             )
             nc.scalar.activation(dst, bank[:], ACT.Square)
 
-        def gaussian_half(dst, b, t, half):
-            square = tile("square%d" % ((2 * (PACK * b + t) + half) % 3), [P, HALF], F32)
-            square_of_d(square[:], b, t, half)
-            nc.scalar.activation(dst, square[:], ACT.Exp, scale=-1.0)
+        def gaussian(b, t, parts):
+            square = tile("square%d" % (t % 2), [P, S], F32)
+            done = 0
+            for dst, j in parts:
+                while done < j.stop:
+                    square_of_d(square[:, done : done + HALF], b, t, done // HALF)
+                    done += HALF
+                nc.scalar.activation(dst, square[:, j], ACT.Exp, scale=-1.0)
 
-        def gaussian(name, b, t):
+        def whole_gaussian(name, b, t):
             plane = tile(name, [P, S], F32)
-            for half in range(2):
-                gaussian_half(plane[:, HALVES[half]], b, t, half)
+            gaussian(b, t, [(plane[:], WHOLE)])
             return plane
 
         def weigh(factor, b, t, j):
@@ -251,18 +254,18 @@ def tile_list_pair_distance_messages_kernel(
             nc.sync.dma_start(bias[:], bm.rearrange("(t p) -> p t", p=P))
 
         quantize_weight(wa_words[1][0], wa_scales[1][0], round_weight(2, wa01, VECTOR))
-        first = gaussian("gauss0", 0, 0)
+        first = tile("gauss0", [P, S], F32)
+        gaussian(0, 0, [(first[:, j], j) for j in HALVES])
         for j in HALVES:
             weigh(first[:, j], 0, 0, j)
         quantize_weight(wa_words[1][1], wa_scales[1][1], round_weight(3, wa11, VECTOR))
         for t in range(1, PACK):
-            weigh(gaussian("gauss%d" % t, 0, t)[:], 0, t, WHOLE)
+            weigh(whole_gaussian("gauss%d" % t, 0, t)[:], 0, t, WHOLE)
 
-        late = [gaussian(name, 1, t) for t, name in enumerate(("v_words0", "v_words1", "v2_words"))]
+        late = [whole_gaussian(name, 1, t) for t, name in enumerate(("v_words0", "v_words1", "v2_words"))]
         last = [tile("gauss%d" % half, [P, HALF], F32) for half in range(2)]
-        for half in range(2):
-            gaussian_half(last[half][:], 1, PACK - 1, half)
-        h0_staged = [round_rows(1 + half, h_planes[0][:, :, HALVES[half]], SCALAR) for half in range(2)]
+        gaussian(1, PACK - 1, [(last[half][:], HALVES[half]) for half in range(2)])
+        h0_staged = [round_rows(1 + half, h_planes[0][:, :, HALVES[half]], (True,)) for half in range(2)]
 
         sums = [
             [ps.tile([P, 2, QUARTER], F32, name="bank%d" % ((4 + 2 * q + pair) % 8)) for pair in range(2)]
@@ -280,7 +283,7 @@ def tile_list_pair_distance_messages_kernel(
             for i in range(2):
                 c = slice(i * QUARTER, (i + 1) * QUARTER)
                 message_pass(0, sums[2 * half + i], wm_words0, words[:, c], scales[:, c])
-        wm1_staged = round_rows(3, wm1[:], SHARED)
+        wm1_staged = round_rows(3, wm1[:], (True,))
 
         quarters = [slice(q * QUARTER, (q + 1) * QUARTER) for q in range(4)]
         for q, j in enumerate(quarters):

@@ -136,26 +136,25 @@ def tile_list_pair_distance_messages_kernel(
         def square_of_d(dst, b, t, half):
             bank = ps.tile([P, HALF], F32, name="bank%d" % (2 * (t % 2) + half))
             j, m = HALVES[half], slice(t * P, (t + 1) * P)
-            for a in range(2):
+            r = b * PASS + t * P
+            atom_passes = [
+                (wa_columns(b, a, t).bitcast(FP8X4), wa_scales[b][a][:, m], atom_words[a], atom_scales[SCALE_ROWS * a :, j])
+                for a in range(2)
+            ]
+            partner_pass = [
+                (wb_words[:, 2 * r : 2 * (r + P)].bitcast(FP4X4), wb_scales[:, r : r + P], partner_words, partner_scales[:, j])
+            ]
+            passes = atom_passes + partner_pass if (b, t) == (0, 0) else partner_pass + atom_passes
+            for i, (weight, weight_scales, words, scales) in enumerate(passes):
                 nc.tensor.matmul_mx(
                     bank[:],
-                    lhsT=wa_columns(b, a, t).bitcast(FP8X4),
-                    lhsT_scale=wa_scales[b][a][:, m],
-                    rhs=atom_words[a][:, j].bitcast(FP8X4),
-                    rhs_scale=atom_scales[SCALE_ROWS * a :, j],
-                    start=(a == 0),
-                    stop=False,
+                    lhsT=weight,
+                    lhsT_scale=weight_scales,
+                    rhs=words[:, j].bitcast(FP8X4),
+                    rhs_scale=scales,
+                    start=(i == 0),
+                    stop=(i == 2),
                 )
-            r = b * PASS + t * P
-            nc.tensor.matmul_mx(
-                bank[:],
-                lhsT=wb_words[:, 2 * r : 2 * (r + P)].bitcast(FP4X4),
-                lhsT_scale=wb_scales[:, r : r + P],
-                rhs=partner_words[:, j].bitcast(FP8X4),
-                rhs_scale=partner_scales[:, j],
-                start=False,
-                stop=True,
-            )
             nc.scalar.activation(dst, bank[:], ACT.Square)
 
         def gaussian(b, t, parts):
@@ -166,6 +165,7 @@ def tile_list_pair_distance_messages_kernel(
                     square_of_d(square[:, done : done + HALF], b, t, done // HALF)
                     done += HALF
                 nc.scalar.activation(dst, square[:, j], ACT.Exp, scale=-1.0)
+            return square
 
         def whole_gaussian(name, b, t):
             plane = tile(name, [P, S], F32)
@@ -191,12 +191,13 @@ def tile_list_pair_distance_messages_kernel(
 
         def finish(name, bank, pair, j, on_scalar):
             result = tile(name, [P, 2, QUARTER], F32)
-            for i in range(2):
-                column = bias[:, 2 * pair + i : 2 * pair + i + 1]
-                if on_scalar:
+            if on_scalar:
+                for i in range(2):
+                    column = bias[:, 2 * pair + i : 2 * pair + i + 1]
                     nc.scalar.activation(result[:, i, :], bank[:, i, :], ACT.Identity, bias=column)
-                else:
-                    nc.vector.tensor_scalar(result[:, i, :], bank[:, i, :], column, None, ALU.add)
+            else:
+                columns = bias[:, 2 * pair : 2 * pair + 2].unsqueeze(2).to_broadcast([P, 2, QUARTER])
+                nc.vector.tensor_tensor(result[:], bank[:], columns, ALU.add)
             nc.sync.dma_start(out_view[:, 2 * pair : 2 * pair + 2, j], result[:])
 
         SCALAR, VECTOR, SHARED = (True, True), (False, False), (True, False)
@@ -263,8 +264,12 @@ def tile_list_pair_distance_messages_kernel(
             weigh(whole_gaussian("gauss%d" % t, 0, t)[:], 0, t, WHOLE)
 
         late = [whole_gaussian(name, 1, t) for t, name in enumerate(("v_words0", "v_words1", "v2_words"))]
-        last = [tile("gauss%d" % half, [P, HALF], F32) for half in range(2)]
-        gaussian(1, PACK - 1, [(last[half][:], HALVES[half]) for half in range(2)])
+        quarters = [slice(q * QUARTER, (q + 1) * QUARTER) for q in range(4)]
+        last_first = tile("gauss0", [P, QUARTER], F32)
+        last_middle = tile("gauss1", [P, HALF], F32)
+        last_square = gaussian(
+            1, PACK - 1, [(last_first[:], quarters[0]), (last_middle[:], slice(QUARTER, QUARTER + HALF))]
+        )
         h0_staged = [round_rows(1 + half, h_planes[0][:, :, HALVES[half]], (True,)) for half in range(2)]
 
         sums = [
@@ -285,17 +290,29 @@ def tile_list_pair_distance_messages_kernel(
                 message_pass(0, sums[2 * half + i], wm_words0, words[:, c], scales[:, c])
         wm1_staged = round_rows(3, wm1[:], (True,))
 
-        quarters = [slice(q * QUARTER, (q + 1) * QUARTER) for q in range(4)]
-        for q, j in enumerate(quarters):
-            weigh(last[q // 2][:, quarters[q % 2]], 1, PACK - 1, j)
-            if q == 1:
-                wm_words1 = tile("gauss0", [P, N], U32)
-                quantize(wm_words1[:], wm_scales[1][:], wm1_staged[:])
-        for q, j in enumerate(quarters):
+        def round_quarter(q, scalar_does):
+            return round_rows(q % 2, h_planes[1][:, :, quarters[q]], scalar_does)
+
+        def last_pass(q, staged):
             words = tile("h1_words%d" % q, [P, QUARTER], U32)
             scales = tile("h1_scales%d" % q, [P, QUARTER], U8)
-            quantize(words[:], scales[:], round_rows(q % 2, h_planes[1][:, :, j], (q < 2,))[:])
+            quantize(words[:], scales[:], staged[:])
             message_pass(1, sums[q], wm_words1, words[:], scales[:])
+
+        weigh(last_first[:], 1, PACK - 1, quarters[0])
+        staged0 = round_quarter(0, (True,))
+        last_end = tile("gauss0", [P, QUARTER], F32)
+        nc.scalar.activation(last_end[:], last_square[:, quarters[3]], ACT.Exp, scale=-1.0)
+        weigh(last_middle[:, 0:QUARTER], 1, PACK - 1, quarters[1])
+        staged1 = round_quarter(1, (True,))
+        weigh(last_middle[:, QUARTER:HALF], 1, PACK - 1, quarters[2])
+        wm_words1 = tile("gauss1", [P, N], U32)
+        quantize(wm_words1[:], wm_scales[1][:], wm1_staged[:])
+        last_pass(0, staged0)
+        weigh(last_end[:], 1, PACK - 1, quarters[3])
+        last_pass(1, staged1)
+        for q in (2, 3):
+            last_pass(q, round_quarter(q, SHARED if q == 2 else (False,)))
         for q, j in enumerate(quarters):
             for pair in range(2):
                 finish("g_rows%d" % (2 * q + pair), sums[q][pair], pair, j, q < 2 or pair == 0)

@@ -83,7 +83,7 @@ def tile_list_pair_distance_messages_kernel(
                 for r in range(SCALE_ROWS):
                     nc.sync.dma_start(dst[r:P:QUADRANT, :], src[0, r::SCALE_ROWS, :].bitcast(I32))
                 return
-            for quad in range(P // QUADRANT):
+            for quad in (0, 2, 1, 3):
                 blocks = src[:, SCALE_ROWS * quad : SCALE_ROWS * (quad + 1), :]
                 nc.sync.dma_start(dst[QUADRANT * quad : QUADRANT * quad + rows, :], blocks.bitcast(I32))
 
@@ -115,14 +115,16 @@ def tile_list_pair_distance_messages_kernel(
                 c = slice(part * PASS // 2, (part + 1) * PASS // 2)
                 quantize(words[:, c], scales[:, c], staged[:, PACK * c.start : PACK * c.stop])
 
-        def round_rows(slot, src, scalar_does):
-            columns = src.shape[2]
-            staged = tile("staged%d" % slot, [P, PACK * columns], BF16)
-            dst = staged[:].rearrange("p (run e t) -> p run t e", e=RUN, t=PACK)
+        def interleave(dst, src, scalar_does):
+            dst = dst.rearrange("p (run e t) -> p run t e", e=RUN, t=PACK)
+            runs = src.shape[2] // RUN // len(scalar_does)
             src = src.rearrange("p t (run e) -> p run t e", e=RUN)
-            runs = columns // RUN // len(scalar_does)
             for part, on_scalar in enumerate(scalar_does):
                 round_copy(on_scalar, dst[:, part * runs : (part + 1) * runs], src[:, part * runs : (part + 1) * runs])
+
+        def round_rows(name, src, scalar_does):
+            staged = tile(name, [P, PACK * src.shape[2]], BF16)
+            interleave(staged[:], src, scalar_does)
             return staged
 
         def quantize(words, scales, src):
@@ -176,19 +178,6 @@ def tile_list_pair_distance_messages_kernel(
             window = g_rows[PACK * b + t][:].indirect(entries(atoms, j))
             nc.vector.tensor_tensor(h_planes[b][:, t, j], window, factor, ALU.mult)
 
-        def message_pass(b, sums, w_words, words, scales):
-            for t in range(PACK):
-                m = slice(t * P, (t + 1) * P)
-                nc.tensor.matmul_mx(
-                    sums[t // 2][:, t % 2, :],
-                    lhsT=w_words[:, m].bitcast(FP8X4),
-                    lhsT_scale=wm_scales[b][:, m],
-                    rhs=words.bitcast(FP8X4),
-                    rhs_scale=scales,
-                    start=(b == 0 and t % 2 == 0),
-                    stop=(b == 1 and t % 2 == 1),
-                )
-
         def finish(name, bank, pair, j, on_scalar):
             result = tile(name, [P, 2, QUARTER], F32)
             if on_scalar:
@@ -200,7 +189,7 @@ def tile_list_pair_distance_messages_kernel(
                 nc.vector.tensor_tensor(result[:], bank[:], columns, ALU.add)
             nc.sync.dma_start(out_view[:, 2 * pair : 2 * pair + 2, j], result[:])
 
-        SCALAR, VECTOR, SHARED = (True, True), (False, False), (True, False)
+        SCALAR, VECTOR, SHARED = (True, True), (False, False), (False, True)
 
         nc.vector.memset(v_scales[:], 0)
         nc.gpsimd.memset(v2_scales[:], 0)
@@ -245,12 +234,10 @@ def tile_list_pair_distance_messages_kernel(
 
         for t in range(1, PACK):
             load_g(0, t)
-        load_g(1, 0)
+        for t in range(PACK):
+            load_g(1, t)
         wm0 = load_weight(0, wm, 0, 0)
-        load_g(1, 1)
-        load_g(1, 2)
         wm1 = load_weight(1, wm, 1, 0)
-        load_g(1, 3)
         with nc.allow_non_contiguous_dma(reason="one bias value for each partition and output tile"):
             nc.sync.dma_start(bias[:], bm.rearrange("(t p) -> p t", p=P))
 
@@ -263,56 +250,79 @@ def tile_list_pair_distance_messages_kernel(
         for t in range(1, PACK):
             weigh(whole_gaussian("gauss%d" % t, 0, t)[:], 0, t, WHOLE)
 
-        late = [whole_gaussian(name, 1, t) for t, name in enumerate(("v_words0", "v_words1", "v2_words"))]
         quarters = [slice(q * QUARTER, (q + 1) * QUARTER) for q in range(4)]
+        late = [whole_gaussian(name, 1, t) for t, name in enumerate(("v_words0", "v_words1", "v2_words"))]
         last_first = tile("gauss0", [P, QUARTER], F32)
-        last_middle = tile("gauss1", [P, HALF], F32)
-        last_square = gaussian(
-            1, PACK - 1, [(last_first[:], quarters[0]), (last_middle[:], slice(QUARTER, QUARTER + HALF))]
-        )
-        h0_staged = [round_rows(1 + half, h_planes[0][:, :, HALVES[half]], (True,)) for half in range(2)]
+        last_rest = tile("gauss2", [P, S - QUARTER], F32)
+        gaussian(1, PACK - 1, [(last_first[:], quarters[0]), (last_rest[:], slice(QUARTER, S))])
+        h0_first = round_rows("staged0", h_planes[0][:, :, HALVES[0]], (True,))
+        h0_third = round_rows("square0", h_planes[0][:, :, quarters[2]], (True,))
 
-        sums = [
-            [ps.tile([P, 2, QUARTER], F32, name="bank%d" % ((4 + 2 * q + pair) % 8)) for pair in range(2)]
-            for q in range(4)
-        ]
-        weigh(late[0][:], 1, 0, WHOLE)
-        wm_words0 = tile("wm_words0", [P, N], U32)
-        quantize_weight(wm_words0, wm_scales[0], round_rows(0, wm0[:], VECTOR))
-        for t in (1, 2):
+        def mx_tiles(name, columns, words_name=None):
+            return tile(words_name or name + "_words", [P, columns], U32), tile(name + "_scales", [P, columns], U8)
+
+        def round_quarter(staged, q, on_scalar):
+            dst = staged[:, PACK * QUARTER * (q % 2) : PACK * QUARTER * (q % 2 + 1)]
+            interleave(dst, h_planes[1][:, :, quarters[q]], (on_scalar,))
+            return dst
+
+        for t in range(PACK - 1):
             weigh(late[t][:], 1, t, WHOLE)
-        for half, name in enumerate(("v2_words", "g_rows6")):
-            words = tile(name, [P, HALF], U32)
-            scales = tile("h0_scales%d" % half, [P, HALF], U8)
-            quantize(words[:], scales[:], h0_staged[half][:])
-            for i in range(2):
-                c = slice(i * QUARTER, (i + 1) * QUARTER)
-                message_pass(0, sums[2 * half + i], wm_words0, words[:, c], scales[:, c])
-        wm1_staged = round_rows(3, wm1[:], (True,))
-
-        def round_quarter(q, scalar_does):
-            return round_rows(q % 2, h_planes[1][:, :, quarters[q]], scalar_does)
-
-        def last_pass(q, staged):
-            words = tile("h1_words%d" % q, [P, QUARTER], U32)
-            scales = tile("h1_scales%d" % q, [P, QUARTER], U8)
-            quantize(words[:], scales[:], staged[:])
-            message_pass(1, sums[q], wm_words1, words[:], scales[:])
-
         weigh(last_first[:], 1, PACK - 1, quarters[0])
-        staged0 = round_quarter(0, (True,))
-        last_end = tile("gauss0", [P, QUARTER], F32)
-        nc.scalar.activation(last_end[:], last_square[:, quarters[3]], ACT.Exp, scale=-1.0)
-        weigh(last_middle[:, 0:QUARTER], 1, PACK - 1, quarters[1])
-        staged1 = round_quarter(1, (True,))
-        weigh(last_middle[:, QUARTER:HALF], 1, PACK - 1, quarters[2])
-        wm_words1 = tile("gauss1", [P, N], U32)
-        quantize(wm_words1[:], wm_scales[1][:], wm1_staged[:])
-        last_pass(0, staged0)
-        weigh(last_end[:], 1, PACK - 1, quarters[3])
-        last_pass(1, staged1)
-        for q in (2, 3):
-            last_pass(q, round_quarter(q, SHARED if q == 2 else (False,)))
-        for q, j in enumerate(quarters):
+        weigh(last_rest[:, quarters[0]], 1, PACK - 1, quarters[1])
+        h1_first = tile("staged1", [P, PACK * HALF], BF16)
+        rounded = [round_quarter(h1_first, q, True) for q in range(2)]
+        h0_words, h0_scales = mx_tiles("h0_first", HALF, "gauss0")
+        quantize(h0_words[:], h0_scales[:], h0_first[:])
+        h1_words, h1_scales = mx_tiles("h1_first", HALF)
+        for q in range(2):
+            quantize(h1_words[:, quarters[q]], h1_scales[:, quarters[q]], rounded[q])
+            weigh(last_rest[:, quarters[1 + q]], 1, PACK - 1, quarters[2 + q])
+
+        parts = (slice(0, N // 2), slice(N // 2, N))
+        wm0_staged = round_rows("staged2", wm0[:], SHARED)
+        h0_fourth = round_rows("weight_in0", h_planes[0][:, :, quarters[3]], (True,))
+        wm1_staged = round_rows("staged3", wm1[:], VECTOR)
+        wm_words = [
+            [tile("wm_words0", [P, N // 2], U32), tile("weight_in1", [P, N // 2], U32)],
+            [tile("wm_words1", [P, N // 2], U32), tile("gauss3", [P, N // 2], U32)],
+        ]
+        for part, c in enumerate(parts):
+            for b, staged in enumerate((wm0_staged, wm1_staged)):
+                quantize(wm_words[b][part][:], wm_scales[b][:, c], staged[:, PACK * c.start : PACK * c.stop])
+        third = round_rows("square1", h_planes[1][:, :, quarters[2]], (True,))
+
+        def message_pass(bank, b, t, words, scales, start, stop):
+            m = slice(t * P, (t + 1) * P)
+            nc.tensor.matmul_mx(
+                bank,
+                lhsT=wm_words[b][t // 2][:, (t % 2) * P : (t % 2 + 1) * P].bitcast(FP8X4),
+                lhsT_scale=wm_scales[b][:, m],
+                rhs=words.bitcast(FP8X4),
+                rhs_scale=scales,
+                start=start,
+                stop=stop,
+            )
+
+        for t in range(PACK):
+            bank = ps.tile([P, HALF], F32, name="bank%d" % (PACK + t))
+            message_pass(bank[:], 0, t, h0_words[:], h0_scales[:], True, False)
+            message_pass(bank[:], 1, t, h1_words[:], h1_scales[:], False, True)
+            result = tile("g_rows%d" % t, [P, HALF], F32)
+            nc.scalar.activation(result[:], bank[:], ACT.Identity, bias=bias[:, t : t + 1])
+            nc.sync.dma_start(out_view[:, t, HALVES[0]], result[:])
+
+        fourth = round_rows("staged2", h_planes[1][:, :, quarters[3]], (False,))
+        h0_words, h0_scales = mx_tiles("h0_second", HALF, "staged3")
+        for q, h0_staged in enumerate((h0_third, h0_fourth)):
+            quantize(h0_words[:, quarters[q]], h0_scales[:, quarters[q]], h0_staged[:])
+        for q, rounded in enumerate((third[:], fourth[:])):
+            words, scales = mx_tiles("h1_quarter%d" % q, QUARTER, ("weight_in0", None)[q])
+            quantize(words[:], scales[:], rounded)
+            sums = [ps.tile([P, 2, QUARTER], F32, name="bank%d" % (2 * q + pair)) for pair in range(2)]
+            for b, (w, sc) in enumerate(((h0_words[:, quarters[q]], h0_scales[:, quarters[q]]), (words[:], scales[:]))):
+                for i in range(2):
+                    for pair in range(2):
+                        message_pass(sums[pair][:, i, :], b, 2 * pair + i, w, sc, (b, i) == (0, 0), (b, i) == (1, 1))
             for pair in range(2):
-                finish("g_rows%d" % (2 * q + pair), sums[q][pair], pair, j, q < 2 or pair == 0)
+                finish("g_rows%d" % (PACK + 2 * q + pair), sums[pair], pair, quarters[2 + q], pair == 0)

@@ -62,7 +62,8 @@ def tile_list_pair_distance_messages_kernel(
         wa_scales = [tiles("wa_scales%d" % b, 2, [P, PASS], U8) for b in range(2)]
         wm_scales = tiles("wm_scales", 2, [P, N], U8)
         g_rows = tiles("g_rows", 2 * PACK, [P, T], F32)
-        h_planes = tiles("h_planes", 2, [P, PACK, S], F32)
+        h_rows = tiles("h_planes", 2, [P, PACK * S], F32)
+        h_planes = [row[:].rearrange("p (t j) -> p t j", t=PACK) for row in h_rows]
         bias = tile("bias", [P, PACK], F32)
 
         g_view = gT.rearrange("(b p t) c -> b t p c", p=P, t=PACK)
@@ -85,7 +86,8 @@ def tile_list_pair_distance_messages_kernel(
                 return
             for quad in (0, 2, 1, 3):
                 blocks = src[:, SCALE_ROWS * quad : SCALE_ROWS * (quad + 1), :]
-                nc.sync.dma_start(dst[QUADRANT * quad : QUADRANT * quad + rows, :], blocks.bitcast(I32))
+                first_row = QUADRANT * quad + SCALE_ROWS
+                nc.sync.dma_start(dst[first_row : first_row + rows, :], blocks.bitcast(I32))
 
         def load_weight(slot, w, a, b):
             dst = tile("weight_in%d" % slot, [P, PACK, PASS], F32)
@@ -140,7 +142,7 @@ def tile_list_pair_distance_messages_kernel(
             j, m = HALVES[half], slice(t * P, (t + 1) * P)
             r = b * PASS + t * P
             atom_passes = [
-                (wa_columns(b, a, t).bitcast(FP8X4), wa_scales[b][a][:, m], atom_words[a], atom_scales[SCALE_ROWS * a :, j])
+                (wa_columns(b, a, t).bitcast(FP8X4), wa_scales[b][a][:, m], atom_words[a], atom_scales[SCALE_ROWS * (a + 1) :, j])
                 for a in range(2)
             ]
             partner_pass = [
@@ -274,23 +276,27 @@ def tile_list_pair_distance_messages_kernel(
         rounded = [round_quarter(h1_first, q, True) for q in range(2)]
         h0_words, h0_scales = mx_tiles("h0_first", HALF, "gauss0")
         quantize(h0_words[:], h0_scales[:], h0_first[:])
+        weigh(last_rest[:, quarters[1]], 1, PACK - 1, quarters[2])
         h1_words, h1_scales = mx_tiles("h1_first", HALF)
-        for q in range(2):
-            quantize(h1_words[:, quarters[q]], h1_scales[:, quarters[q]], rounded[q])
-            weigh(last_rest[:, quarters[1 + q]], 1, PACK - 1, quarters[2 + q])
-
-        parts = (slice(0, N // 2), slice(N // 2, N))
+        quantize(h1_words[:, quarters[0]], h1_scales[:, quarters[0]], rounded[0])
         wm0_staged = round_rows("staged2", wm0[:], SHARED)
-        h0_fourth = round_rows("weight_in0", h_planes[0][:, :, quarters[3]], (True,))
-        wm1_staged = round_rows("staged3", wm1[:], VECTOR)
-        wm_words = [
-            [tile("wm_words0", [P, N // 2], U32), tile("weight_in1", [P, N // 2], U32)],
-            [tile("wm_words1", [P, N // 2], U32), tile("gauss3", [P, N // 2], U32)],
-        ]
-        for part, c in enumerate(parts):
-            for b, staged in enumerate((wm0_staged, wm1_staged)):
-                quantize(wm_words[b][part][:], wm_scales[b][:, c], staged[:, PACK * c.start : PACK * c.stop])
-        third = round_rows("square1", h_planes[1][:, :, quarters[2]], (True,))
+        quantize(h1_words[:, quarters[1]], h1_scales[:, quarters[1]], rounded[1])
+        first_pair, second_pair = slice(0, 2 * P), slice(2 * P, N)
+        wm0_first = tile("wm_words0", [P, 2 * P], U32)
+        quantize(wm0_first[:], wm_scales[0][:, first_pair], wm0_staged[:, 0 : PACK * 2 * P])
+        wm1_staged = [tile("square1", [P, PACK * P], BF16)[:], h_rows[1][:, PACK * S - QUARTER :].bitcast(BF16)]
+        wm1_words = tile("wm_words1", [P, N], U32)
+        for t in range(2):
+            interleave(wm1_staged[t], wm1[:, :, t * P : (t + 1) * P], (False,))
+        wm1_second = round_rows("staged3", wm1[:, :, second_pair], (True,))
+        h0_fourth = round_rows("weight_in1", h_planes[0][:, :, quarters[3]], (True,))
+        for t in range(2):
+            quantize(wm1_words[:, t * P : (t + 1) * P], wm_scales[1][:, t * P : (t + 1) * P], wm1_staged[t])
+        wm0_second = tile("square1", [P, 2 * P], U32)
+        quantize(wm0_second[:], wm_scales[0][:, second_pair], wm0_staged[:, PACK * 2 * P :])
+        weigh(last_rest[:, quarters[2]], 1, PACK - 1, quarters[3])
+        quantize(wm1_words[:, second_pair], wm_scales[1][:, second_pair], wm1_second[:])
+        wm_words = [[wm0_first[:], wm0_second[:]], [wm1_words[:, first_pair], wm1_words[:, second_pair]]]
 
         def message_pass(bank, b, t, words, scales, start, stop):
             m = slice(t * P, (t + 1) * P)
@@ -312,13 +318,17 @@ def tile_list_pair_distance_messages_kernel(
             nc.scalar.activation(result[:], bank[:], ACT.Identity, bias=bias[:, t : t + 1])
             nc.sync.dma_start(out_view[:, t, HALVES[0]], result[:])
 
-        fourth = round_rows("staged2", h_planes[1][:, :, quarters[3]], (False,))
         h0_words, h0_scales = mx_tiles("h0_second", HALF, "staged3")
-        for q, h0_staged in enumerate((h0_third, h0_fourth)):
-            quantize(h0_words[:, quarters[q]], h0_scales[:, quarters[q]], h0_staged[:])
-        for q, rounded in enumerate((third[:], fourth[:])):
-            words, scales = mx_tiles("h1_quarter%d" % q, QUARTER, ("weight_in0", None)[q])
-            quantize(words[:], scales[:], rounded)
+        late_rounded = []
+        for q, (name, h0_staged) in enumerate((("staged2", h0_third), ("staged0", h0_fourth))):
+            late_rounded.append(round_rows(name, h_planes[1][:, :, quarters[2 + q]], (False,)))
+            if q == 0:
+                quantize(h0_words[:, quarters[q]], h0_scales[:, quarters[q]], h0_staged[:])
+        for q in range(2):
+            words, scales = mx_tiles("h1_quarter%d" % q, QUARTER)
+            if q == 1:
+                quantize(h0_words[:, quarters[q]], h0_scales[:, quarters[q]], h0_fourth[:])
+            quantize(words[:], scales[:], late_rounded[q][:])
             sums = [ps.tile([P, 2, QUARTER], F32, name="bank%d" % (2 * q + pair)) for pair in range(2)]
             for b, (w, sc) in enumerate(((h0_words[:, quarters[q]], h0_scales[:, quarters[q]]), (words[:], scales[:]))):
                 for i in range(2):

@@ -134,7 +134,7 @@ def tile_list_pair_distance_messages_kernel(
 
         def wa_columns(b, a, t):
             if (b, a) == (0, 1) and t >= 2:
-                return late_words[:, (t - 2) * P : (t - 1) * P]
+                return held_words[:, (t - 2) * P : (t - 1) * P]
             return wa_words[b][a][:, t * P : (t + 1) * P]
 
         def square_of_d(dst, b, t, half):
@@ -148,7 +148,7 @@ def tile_list_pair_distance_messages_kernel(
             partner_pass = [
                 (wb_words[:, 2 * r : 2 * (r + P)].bitcast(FP4X4), wb_scales[:, r : r + P], partner_words, partner_scales[:, j])
             ]
-            passes = atom_passes + partner_pass if (b, t) == (0, 0) else partner_pass + atom_passes
+            passes = atom_passes + partner_pass if b == 0 and t + half < 2 else partner_pass + atom_passes
             for i, (weight, weight_scales, words, scales) in enumerate(passes):
                 nc.tensor.matmul_mx(
                     bank[:],
@@ -161,19 +161,15 @@ def tile_list_pair_distance_messages_kernel(
                 )
             nc.scalar.activation(dst, bank[:], ACT.Square)
 
-        def gaussian(b, t, parts):
-            square = tile("square%d" % (t % 2), [P, S], F32)
-            done = 0
-            for dst, j in parts:
-                while done < j.stop:
-                    square_of_d(square[:, done : done + HALF], b, t, done // HALF)
-                    done += HALF
-                nc.scalar.activation(dst, square[:, j], ACT.Exp, scale=-1.0)
-            return square
+        def squares_of_pair(b, pair, order):
+            squares = tiles("square", 2, [P, S], F32)
+            for i, half in order:
+                square_of_d(squares[i][:, HALVES[half]], b, 2 * pair + i, half)
+            return squares
 
-        def whole_gaussian(name, b, t):
-            plane = tile(name, [P, S], F32)
-            gaussian(b, t, [(plane[:], WHOLE)])
+        def gaussian(name, square, j):
+            plane = tile(name, [P, j.stop - j.start], F32)
+            nc.scalar.activation(plane[:], square[:, j], ACT.Exp, scale=-1.0)
             return plane
 
         def weigh(factor, b, t, j):
@@ -231,8 +227,6 @@ def tile_list_pair_distance_messages_kernel(
         quantize(wa_words[0][1][:, 0:half_pass], wa_scales[0][1][:, 0:half_pass], staged[:, 0 : PACK * half_pass])
         for j in HALVES:
             pick(partner_words, v2_words, U32, partners, j)
-        late_words = tile("v2_words", [P, half_pass], U32)
-        quantize(late_words[:], wa_scales[0][1][:, half_pass:], staged[:, PACK * half_pass :])
 
         for t in range(1, PACK):
             load_g(0, t)
@@ -244,21 +238,35 @@ def tile_list_pair_distance_messages_kernel(
             nc.sync.dma_start(bias[:], bm.rearrange("(t p) -> p t", p=P))
 
         quantize_weight(wa_words[1][0], wa_scales[1][0], round_weight(2, wa01, VECTOR))
+        held_words = tile("weight_in2", [P, half_pass], U32)
+        quantize(held_words[:], wa_scales[0][1][:, half_pass:], staged[:, PACK * half_pass :])
         first = tile("gauss0", [P, S], F32)
-        gaussian(0, 0, [(first[:, j], j) for j in HALVES])
+        squares = tiles("square", 2, [P, S], F32)
+        for half, j in enumerate(HALVES):
+            for t in range(2):
+                square_of_d(squares[t][:, j], 0, t, half)
+            nc.scalar.activation(first[:, j], squares[0][:, j], ACT.Exp, scale=-1.0)
+        second = gaussian("gauss1", squares[1], WHOLE)
         for j in HALVES:
             weigh(first[:, j], 0, 0, j)
         quantize_weight(wa_words[1][1], wa_scales[1][1], round_weight(3, wa11, VECTOR))
-        for t in range(1, PACK):
-            weigh(whole_gaussian("gauss%d" % t, 0, t)[:], 0, t, WHOLE)
+        weigh(second[:], 0, 1, WHOLE)
+        by_plane = [(i, half) for i in range(2) for half in range(2)]
+        for i, square in enumerate(squares_of_pair(0, 1, by_plane)):
+            weigh(gaussian("gauss%d" % (2 + i), square, WHOLE)[:], 0, 2 + i, WHOLE)
 
         quarters = [slice(q * QUARTER, (q + 1) * QUARTER) for q in range(4)]
-        late = [whole_gaussian(name, 1, t) for t, name in enumerate(("v_words0", "v_words1", "v2_words"))]
-        last_first = tile("gauss0", [P, QUARTER], F32)
-        last_rest = tile("gauss2", [P, S - QUARTER], F32)
-        gaussian(1, PACK - 1, [(last_first[:], quarters[0]), (last_rest[:], slice(QUARTER, S))])
+        late = [gaussian("v_words%d" % i, square, WHOLE) for i, square in enumerate(squares_of_pair(1, 0, by_plane))]
+        squares = squares_of_pair(1, 1, by_plane)
+        late.append(gaussian("v2_words", squares[0], WHOLE))
+        last_first = gaussian("gauss0", squares[1], quarters[0])
+        last_second = gaussian("gauss1", squares[1], quarters[1])
+        last_rest = gaussian("gauss2", squares[1], HALVES[1])
         h0_first = round_rows("staged0", h_planes[0][:, :, HALVES[0]], (True,))
-        h0_third = round_rows("square0", h_planes[0][:, :, quarters[2]], (True,))
+        eighth = QUARTER // 2
+        h0_second = tile("staged3", [P, PACK * HALF], BF16)
+        interleave(h0_second[:, 0 : PACK * (HALF - eighth)], h_planes[0][:, :, HALF : S - eighth], (True,))
+        h0_third, h0_fourth = h0_second[:, 0 : PACK * QUARTER], h0_second[:, PACK * QUARTER : PACK * HALF]
 
         def mx_tiles(name, columns, words_name=None):
             return tile(words_name or name + "_words", [P, columns], U32), tile(name + "_scales", [P, columns], U8)
@@ -271,30 +279,49 @@ def tile_list_pair_distance_messages_kernel(
         for t in range(PACK - 1):
             weigh(late[t][:], 1, t, WHOLE)
         weigh(last_first[:], 1, PACK - 1, quarters[0])
-        weigh(last_rest[:, quarters[0]], 1, PACK - 1, quarters[1])
+        weigh(last_second[:], 1, PACK - 1, quarters[1])
         h1_first = tile("staged1", [P, PACK * HALF], BF16)
         rounded = [round_quarter(h1_first, q, True) for q in range(2)]
         h0_words, h0_scales = mx_tiles("h0_first", HALF, "gauss0")
         quantize(h0_words[:], h0_scales[:], h0_first[:])
-        weigh(last_rest[:, quarters[1]], 1, PACK - 1, quarters[2])
+        weigh(last_rest[:, quarters[0]], 1, PACK - 1, quarters[2])
+        late_words, late_scales = mx_tiles("h0_second", HALF, "gauss1")
+        quantize(late_words[:, quarters[0]], late_scales[:, quarters[0]], h0_third)
+        idle_bank = ps.tile([P, HALF], F32, name="bank0")
+        for unused in range(5):
+            nc.tensor.matmul_mx(
+                idle_bank[:, quarters[0]],
+                lhsT=wa_words[1][1][:, 0:P].bitcast(FP8X4),
+                lhsT_scale=wa_scales[1][1][:, 0:P],
+                rhs=late_words[:, quarters[0]].bitcast(FP8X4),
+                rhs_scale=late_scales[:, quarters[0]],
+                start=True,
+                stop=True,
+            )
         h1_words, h1_scales = mx_tiles("h1_first", HALF)
         quantize(h1_words[:, quarters[0]], h1_scales[:, quarters[0]], rounded[0])
-        wm0_staged = round_rows("staged2", wm0[:], SHARED)
-        quantize(h1_words[:, quarters[1]], h1_scales[:, quarters[1]], rounded[1])
         first_pair, second_pair = slice(0, 2 * P), slice(2 * P, N)
+        wm0_rounded = round_rows("staged2", wm0[:], SHARED)
+        wm0_staged = [wm0_rounded[:, 0 : PACK * 2 * P], wm0_rounded[:, PACK * 2 * P :]]
+        quantize(h1_words[:, quarters[1]], h1_scales[:, quarters[1]], rounded[1])
         wm0_first = tile("wm_words0", [P, 2 * P], U32)
-        quantize(wm0_first[:], wm_scales[0][:, first_pair], wm0_staged[:, 0 : PACK * 2 * P])
-        wm1_staged = [tile("square1", [P, PACK * P], BF16)[:], h_rows[1][:, PACK * S - QUARTER :].bitcast(BF16)]
+        quantize(wm0_first[:], wm_scales[0][:, first_pair], wm0_staged[0])
+        h0_end = h0_second[:, PACK * (HALF - eighth) :]
+        wm1_pieces = [
+            (h0_end[:, 0 : PACK * P // 2], slice(0, P // 2)),
+            (tile("square1", [P, PACK * P // 2], BF16)[:], slice(P // 2, P)),
+            (h_rows[1][:, PACK * S - QUARTER :].bitcast(BF16), slice(P, 2 * P)),
+        ]
         wm1_words = tile("wm_words1", [P, N], U32)
-        for t in range(2):
-            interleave(wm1_staged[t], wm1[:, :, t * P : (t + 1) * P], (False,))
-        wm1_second = round_rows("staged3", wm1[:, :, second_pair], (True,))
-        h0_fourth = round_rows("weight_in1", h_planes[0][:, :, quarters[3]], (True,))
-        for t in range(2):
-            quantize(wm1_words[:, t * P : (t + 1) * P], wm_scales[1][:, t * P : (t + 1) * P], wm1_staged[t])
+        for staged, c in wm1_pieces:
+            interleave(staged, wm1[:, :, c], (False,))
+        wm1_second = round_rows("square0", wm1[:, :, second_pair], (True,))
+        for staged, c in wm1_pieces:
+            quantize(wm1_words[:, c], wm_scales[1][:, c], staged)
+        interleave(h0_end, h_planes[0][:, :, S - eighth :], (True,))
         wm0_second = tile("square1", [P, 2 * P], U32)
-        quantize(wm0_second[:], wm_scales[0][:, second_pair], wm0_staged[:, PACK * 2 * P :])
-        weigh(last_rest[:, quarters[2]], 1, PACK - 1, quarters[3])
+        quantize(wm0_second[:], wm_scales[0][:, second_pair], wm0_staged[1])
+        weigh(last_rest[:, quarters[1]], 1, PACK - 1, quarters[3])
         quantize(wm1_words[:, second_pair], wm_scales[1][:, second_pair], wm1_second[:])
         wm_words = [[wm0_first[:], wm0_second[:]], [wm1_words[:, first_pair], wm1_words[:, second_pair]]]
 
@@ -318,21 +345,21 @@ def tile_list_pair_distance_messages_kernel(
             nc.scalar.activation(result[:], bank[:], ACT.Identity, bias=bias[:, t : t + 1])
             nc.sync.dma_start(out_view[:, t, HALVES[0]], result[:])
 
-        h0_words, h0_scales = mx_tiles("h0_second", HALF, "staged3")
-        late_rounded = []
-        for q, (name, h0_staged) in enumerate((("staged2", h0_third), ("staged0", h0_fourth))):
-            late_rounded.append(round_rows(name, h_planes[1][:, :, quarters[2 + q]], (False,)))
-            if q == 0:
-                quantize(h0_words[:, quarters[q]], h0_scales[:, quarters[q]], h0_staged[:])
+        third = round_rows("staged2", h_planes[1][:, :, quarters[2]], (False,))
+        fourth_words = tile("gauss2", [P, QUARTER], U32)
+        quantize(fourth_words[:], late_scales[:, quarters[1]], h0_fourth)
+        sums = [[ps.tile([P, 2, QUARTER], F32, name="bank%d" % (2 * q + pair)) for pair in range(2)] for q in range(2)]
+
+        def quarter_pass(q, b, words, scales):
+            for i in range(2):
+                for pair in range(2):
+                    message_pass(sums[q][pair][:, i, :], b, 2 * pair + i, words, scales, (b, i) == (0, 0), (b, i) == (1, 1))
+
         for q in range(2):
+            quarter_pass(q, 0, (late_words[:, quarters[0]], fourth_words[:])[q], late_scales[:, quarters[q]])
+            rounded = third if q == 0 else round_rows("staged0", h_planes[1][:, :, quarters[3]], (False,))
             words, scales = mx_tiles("h1_quarter%d" % q, QUARTER)
-            if q == 1:
-                quantize(h0_words[:, quarters[q]], h0_scales[:, quarters[q]], h0_fourth[:])
-            quantize(words[:], scales[:], late_rounded[q][:])
-            sums = [ps.tile([P, 2, QUARTER], F32, name="bank%d" % (2 * q + pair)) for pair in range(2)]
-            for b, (w, sc) in enumerate(((h0_words[:, quarters[q]], h0_scales[:, quarters[q]]), (words[:], scales[:]))):
-                for i in range(2):
-                    for pair in range(2):
-                        message_pass(sums[pair][:, i, :], b, 2 * pair + i, w, sc, (b, i) == (0, 0), (b, i) == (1, 1))
+            quantize(words[:], scales[:], rounded[:])
+            quarter_pass(q, 1, words[:], scales[:])
             for pair in range(2):
-                finish("g_rows%d" % (PACK + 2 * q + pair), sums[pair], pair, quarters[2 + q], pair == 0)
+                finish("g_rows%d" % (PACK + 2 * q + pair), sums[q][pair], pair, quarters[2 + q], pair == 0)

@@ -265,7 +265,7 @@ def tile_list_pair_distance_messages_kernel(
         h0_first = round_rows("staged0", h_planes[0][:, :, HALVES[0]], (True,))
         eighth = QUARTER // 2
         h0_second = tile("staged3", [P, PACK * HALF], BF16)
-        interleave(h0_second[:, 0 : PACK * (HALF - eighth)], h_planes[0][:, :, HALF : S - eighth], (True,))
+        interleave(h0_second[:], h_planes[0][:, :, HALVES[1]], (True,))
         h0_third, h0_fourth = h0_second[:, 0 : PACK * QUARTER], h0_second[:, PACK * QUARTER : PACK * HALF]
 
         def mx_tiles(name, columns, words_name=None):
@@ -306,9 +306,9 @@ def tile_list_pair_distance_messages_kernel(
         quantize(h1_words[:, quarters[1]], h1_scales[:, quarters[1]], rounded[1])
         wm0_first = tile("wm_words0", [P, 2 * P], U32)
         quantize(wm0_first[:], wm_scales[0][:, first_pair], wm0_staged[0])
-        h0_end = h0_second[:, PACK * (HALF - eighth) :]
+        third_end = tile("staged0", [P, PACK * eighth], BF16)
         wm1_pieces = [
-            (h0_end[:, 0 : PACK * P // 2], slice(0, P // 2)),
+            (third_end[:, 0 : PACK * P // 2], slice(0, P // 2)),
             (tile("square1", [P, PACK * P // 2], BF16)[:], slice(P // 2, P)),
             (h_rows[1][:, PACK * S - QUARTER :].bitcast(BF16), slice(P, 2 * P)),
         ]
@@ -318,7 +318,7 @@ def tile_list_pair_distance_messages_kernel(
         wm1_second = round_rows("square0", wm1[:, :, second_pair], (True,))
         for staged, c in wm1_pieces:
             quantize(wm1_words[:, c], wm_scales[1][:, c], staged)
-        interleave(h0_end, h_planes[0][:, :, S - eighth :], (True,))
+        interleave(third_end[:], h_planes[1][:, :, HALF + eighth : HALF + QUARTER], (True,))
         wm0_second = tile("square1", [P, 2 * P], U32)
         quantize(wm0_second[:], wm_scales[0][:, second_pair], wm0_staged[1])
         weigh(last_rest[:, quarters[1]], 1, PACK - 1, quarters[3])
@@ -345,7 +345,7 @@ def tile_list_pair_distance_messages_kernel(
             nc.scalar.activation(result[:], bank[:], ACT.Identity, bias=bias[:, t : t + 1])
             nc.sync.dma_start(out_view[:, t, HALVES[0]], result[:])
 
-        third = round_rows("staged2", h_planes[1][:, :, quarters[2]], (False,))
+        third_start = round_rows("staged2", h_planes[1][:, :, HALF : HALF + eighth], (False,))
         fourth_words = tile("gauss2", [P, QUARTER], U32)
         quantize(fourth_words[:], late_scales[:, quarters[1]], h0_fourth)
         sums = [[ps.tile([P, 2, QUARTER], F32, name="bank%d" % (2 * q + pair)) for pair in range(2)] for q in range(2)]
@@ -357,9 +357,14 @@ def tile_list_pair_distance_messages_kernel(
 
         for q in range(2):
             quarter_pass(q, 0, (late_words[:, quarters[0]], fourth_words[:])[q], late_scales[:, quarters[q]])
-            rounded = third if q == 0 else round_rows("staged0", h_planes[1][:, :, quarters[3]], (False,))
+            if q == 0:
+                rounded = (third_end[:], third_start[:])
+            else:
+                fourth = round_rows("staged1", h_planes[1][:, :, quarters[3]], VECTOR)
+                rounded = (fourth[:, PACK * eighth :], fourth[:, 0 : PACK * eighth])
             words, scales = mx_tiles("h1_quarter%d" % q, QUARTER)
-            quantize(words[:], scales[:], rounded[:])
+            for staged, c in zip(rounded[:: 1 - 2 * q], (slice(eighth, QUARTER), slice(0, eighth))[:: 1 - 2 * q]):
+                quantize(words[:, c], scales[:, c], staged)
             quarter_pass(q, 1, words[:], scales[:])
             for pair in range(2):
                 finish("g_rows%d" % (PACK + 2 * q + pair), sums[q][pair], pair, quarters[2 + q], pair == 0)

@@ -284,20 +284,20 @@ def tile_list_pair_distance_messages_kernel(
         rounded = [round_quarter(h1_first, q, True) for q in range(2)]
         h0_words, h0_scales = mx_tiles("h0_first", HALF, "gauss0")
         quantize(h0_words[:], h0_scales[:], h0_first[:])
-        weigh(last_rest[:, quarters[0]], 1, PACK - 1, quarters[2])
-        late_words, late_scales = mx_tiles("h0_second", HALF, "gauss1")
-        quantize(late_words[:, quarters[0]], late_scales[:, quarters[0]], h0_third)
         idle_bank = ps.tile([P, HALF], F32, name="bank0")
-        for unused in range(5):
+        for unused in range(4):
             nc.tensor.matmul_mx(
-                idle_bank[:, quarters[0]],
+                idle_bank[:],
                 lhsT=wa_words[1][1][:, 0:P].bitcast(FP8X4),
                 lhsT_scale=wa_scales[1][1][:, 0:P],
-                rhs=late_words[:, quarters[0]].bitcast(FP8X4),
-                rhs_scale=late_scales[:, quarters[0]],
+                rhs=h0_words[:].bitcast(FP8X4),
+                rhs_scale=h0_scales[:],
                 start=True,
                 stop=True,
             )
+        weigh(last_rest[:, quarters[0]], 1, PACK - 1, quarters[2])
+        late_words, late_scales = mx_tiles("h0_second", HALF, "gauss1")
+        quantize(late_words[:, quarters[0]], late_scales[:, quarters[0]], h0_third)
         h1_words, h1_scales = mx_tiles("h1_first", HALF)
         quantize(h1_words[:, quarters[0]], h1_scales[:, quarters[0]], rounded[0])
         first_pair, second_pair = slice(0, 2 * P), slice(2 * P, N)

@@ -56,9 +56,9 @@ def tile_list_pair_distance_messages_kernel(
         wb_scales = tile("wb_scales", [P, H], U8)
         atom_words = tiles("atom_words", 2, [P, S], U32)
         atom_scales = tile("atom_scales", [P, S], U8)
-        partner_words = tile("partner_words", [P, S], U32)
         partner_scales = tile("partner_scales", [P, S], U8)
-        wa_words = [tiles("wa_words%d" % b, 2, [P, PASS], U32) for b in range(2)]
+        wa_words = tiles("wa_words1", 2, [P, PASS], U32)
+        first_words = {}
         wa_scales = [tiles("wa_scales%d" % b, 2, [P, PASS], U8) for b in range(2)]
         wm_scales = tiles("wm_scales", 2, [P, N], U8)
         g_rows = tiles("g_rows", 2 * PACK, [P, T], F32)
@@ -78,16 +78,17 @@ def tile_list_pair_distance_messages_kernel(
         def load_words(dst, src):
             nc.sync.dma_start(dst[:], src.rearrange("p c i -> p (c i)").bitcast(I32))
 
-        def load_scales(dst, src):
+        def load_scales(dst, src, quads=()):
             rows = SCALE_ROWS * src.shape[0]
             if rows == SCALE_ROWS:
                 for r in range(SCALE_ROWS):
                     nc.sync.dma_start(dst[r:P:QUADRANT, :], src[0, r::SCALE_ROWS, :].bitcast(I32))
                 return
-            for quad in (0, 2, 1, 3):
+            for quad in quads:
                 blocks = src[:, SCALE_ROWS * quad : SCALE_ROWS * (quad + 1), :]
                 first_row = QUADRANT * quad + SCALE_ROWS
-                nc.sync.dma_start(dst[first_row : first_row + rows, :], blocks.bitcast(I32))
+                queue = nc.sync if quad == 3 else nc.gpsimd
+                queue.dma_start(dst[first_row : first_row + rows, :], blocks.bitcast(I32))
 
         def load_weight(slot, w, a, b):
             dst = tile("weight_in%d" % slot, [P, PACK, PASS], F32)
@@ -133,9 +134,9 @@ def tile_list_pair_distance_messages_kernel(
             nc.vector.quantize_mx(out=words.bitcast(FP8X4), scales=scales, in_=src)
 
         def wa_columns(b, a, t):
-            if (b, a) == (0, 1) and t >= 2:
-                return held_words[:, (t - 2) * P : (t - 1) * P]
-            return wa_words[b][a][:, t * P : (t + 1) * P]
+            if b == 0:
+                return first_words[a, t // 2][:, (t % 2) * P : (t % 2 + 1) * P]
+            return wa_words[a][:, t * P : (t + 1) * P]
 
         def square_of_d(dst, b, t, half):
             bank = ps.tile([P, HALF], F32, name="bank%d" % (2 * (t % 2) + half))
@@ -187,44 +188,58 @@ def tile_list_pair_distance_messages_kernel(
                 nc.vector.tensor_tensor(result[:], bank[:], columns, ALU.add)
             nc.sync.dma_start(out_view[:, 2 * pair : 2 * pair + 2, j], result[:])
 
-        SCALAR, VECTOR, SHARED = (True, True), (False, False), (False, True)
+        VECTOR, SHARED = (False, False), (False, True)
 
-        nc.vector.memset(v_scales[:], 0)
-        nc.gpsimd.memset(v2_scales[:], 0)
-        nc.gpsimd.memset(wb_scales_in[:], 0)
+        nc.gpsimd.memset(v_scales[:], 0)
+        nc.vector.memset(v2_scales[:], 0)
+        nc.vector.memset(wb_scales_in[:], 0)
+        load_scales(v_scales, tab_scales, (0, 2, 1))
 
-        nc.sync.dma_start(atoms[:], offs)
-        nc.sync.dma_start(wb_words_in[:], wb4_words[0].bitcast(I32))
-        load_scales(v_scales, tab_scales)
-        load_words(v_words[0], tab_words[0])
         nc.sync.dma_start(partners[:], offs2)
+        nc.sync.dma_start(wb_words_in[:], wb4_words[0].bitcast(I32))
         load_scales(v2_scales, tab2_scales)
-        wa00 = load_weight(0, wa, 0, 0)
+        nc.sync.dma_start(atoms[:], offs)
+        load_words(v_words[0], tab_words[0])
         load_words(v_words[1], tab_words[1])
+        load_scales(v_scales, tab_scales, (3,))
         load_scales(wb_scales_in, wb4_scales)
+        wa00 = load_weight(0, wa, 0, 0)
         wa10 = load_weight(1, wa, 1, 0)
         load_words(v2_words, tab2_words[0])
         wa01 = load_weight(2, wa, 0, 1)
         load_g(0, 0)
         wa11 = load_weight(3, wa, 1, 1)
 
-        pick(atom_scales, v_scales, U8, atoms, WHOLE)
-        pick(atom_words[0], v_words[0], U32, atoms, WHOLE)
-        staged = round_weight(0, wa00, SCALAR)
-        pick(partner_scales, v2_scales, U8, partners, WHOLE)
-        quantize_weight(wa_words[0][0], wa_scales[0][0], staged)
-        pick(atom_words[1], v_words[1], U32, atoms, WHOLE)
-        nc.vector.tensor_copy(
+        half_pass = PASS // 2
+
+        def round_pair(name, src, pair):
+            staged = tile(name, [P, PACK * half_pass], BF16)
+            dst = staged[:].rearrange("p (t m i) -> p m i t", t=2, i=PACK)
+            round_copy(True, dst, src[:].rearrange("p i (m t) -> p m i t", t=PACK)[:, :, :, 2 * pair : 2 * pair + 2])
+            return staged
+
+        def quantize_pair(name, a, pair, staged):
+            words = tile(name, [P, half_pass], U32)
+            quantize(words[:], wa_scales[0][a][:, pair * half_pass : (pair + 1) * half_pass], staged[:])
+            first_words[a, pair] = words
+
+        nc.scalar.copy(
             wb_words[:].bitcast(U16).rearrange("p (b t m) -> p b t m", b=2, t=PACK),
             wb_words_in[:].bitcast(U16).rearrange("p (b m t) -> p b t m", b=2, t=PACK),
         )
+        pick(partner_scales, v2_scales, U8, partners, WHOLE)
+        pick(atom_words[0], v_words[0], U32, atoms, WHOLE)
+        pick(atom_words[1], v_words[1], U32, atoms, WHOLE)
         nc.vector.tensor_copy(
             wb_scales[:].rearrange("p (b t m) -> p b t m", b=2, t=PACK),
             wb_scales_in[:].bitcast(U8).rearrange("p (b m t) -> p b t m", b=2, t=PACK),
         )
-        staged = round_weight(1, wa10, SCALAR)
-        half_pass = PASS // 2
-        quantize(wa_words[0][1][:, 0:half_pass], wa_scales[0][1][:, 0:half_pass], staged[:, 0 : PACK * half_pass])
+        pick(atom_scales, v_scales, U8, atoms, WHOLE)
+        pieces = [round_pair("staged0", wa00, 0), round_pair("pair1", wa00, 1), round_pair("pair2", wa10, 0), round_pair("staged1", wa10, 1)]
+        quantize_pair("v_scales", 0, 0, pieces[0])
+        quantize_pair("wa_words001", 0, 1, pieces[1])
+        quantize_pair("wa_words010", 1, 0, pieces[2])
+        partner_words = tile("pair1", [P, S], U32)
         for j in HALVES:
             pick(partner_words, v2_words, U32, partners, j)
 
@@ -237,9 +252,8 @@ def tile_list_pair_distance_messages_kernel(
         with nc.allow_non_contiguous_dma(reason="one bias value for each partition and output tile"):
             nc.sync.dma_start(bias[:], bm.rearrange("(t p) -> p t", p=P))
 
-        quantize_weight(wa_words[1][0], wa_scales[1][0], round_weight(2, wa01, VECTOR))
-        held_words = tile("weight_in2", [P, half_pass], U32)
-        quantize(held_words[:], wa_scales[0][1][:, half_pass:], staged[:, PACK * half_pass :])
+        quantize_weight(wa_words[0], wa_scales[1][0], round_weight(2, wa01, VECTOR))
+        quantize_pair("weight_in2", 1, 1, pieces[3])
         first = tile("gauss0", [P, S], F32)
         squares = tiles("square", 2, [P, S], F32)
         for half, j in enumerate(HALVES):
@@ -249,7 +263,7 @@ def tile_list_pair_distance_messages_kernel(
         second = gaussian("gauss1", squares[1], WHOLE)
         for j in HALVES:
             weigh(first[:, j], 0, 0, j)
-        quantize_weight(wa_words[1][1], wa_scales[1][1], round_weight(3, wa11, VECTOR))
+        quantize_weight(wa_words[1], wa_scales[1][1], round_weight(3, wa11, VECTOR))
         weigh(second[:], 0, 1, WHOLE)
         by_plane = [(i, half) for i in range(2) for half in range(2)]
         for i, square in enumerate(squares_of_pair(0, 1, by_plane)):
@@ -288,7 +302,7 @@ def tile_list_pair_distance_messages_kernel(
         for unused in range(4):
             nc.tensor.matmul_mx(
                 idle_bank[:],
-                lhsT=wa_words[1][1][:, 0:P].bitcast(FP8X4),
+                lhsT=wa_words[1][:, 0:P].bitcast(FP8X4),
                 lhsT_scale=wa_scales[1][1][:, 0:P],
                 rhs=h0_words[:].bitcast(FP8X4),
                 rhs_scale=h0_scales[:],

from contextlib import ExitStack

import concourse.mybir as mybir

K, Q, H, N, T, S = 1024, 512, 1024, 512, 2048, 1024
FLOPS = 2 * S * (K * H + Q * H + H * N)

F32 = mybir.dt.float32
BF16 = mybir.dt.bfloat16
I32 = mybir.dt.int32
U32 = mybir.dt.uint32
U16 = mybir.dt.uint16
U8 = mybir.dt.uint8
FP8X4 = mybir.dt.float8_e4m3fn_x4
FP4X4 = mybir.dt.float4_e2m1fn_x4
ACT = mybir.ActivationFunctionType
ALU = mybir.AluOpType

P = 128
PACK = 4
PASS = P * PACK
HALF = 512
QUADRANT = 32
SCALE_ROWS = 4
I32_BYTES = 4
PER_COLUMN = 16
HALVES = (slice(0, HALF), slice(HALF, S))
WHOLE = slice(0, S)
QUARTER = HALF // 2
RUN = 2


def tile_list_pair_distance_messages_kernel(
    tc, tab_words, tab_scales, tab2_words, tab2_scales, offs, offs2, wa, wb4_words, wb4_scales, gT, wm, bm, out
):
    nc = tc.nc
    with ExitStack() as ctx:
        sb = ctx.enter_context(tc.tile_pool(name="sb", bufs=1))
        ps = ctx.enter_context(tc.psum_pool(name="ps", bufs=1))

        def tile(name, shape, dtype):
            return sb.tile(shape, dtype, name=name, align_bytes=64)

        def tiles(name, count, shape, dtype):
            return [tile("%s%d" % (name, i), shape, dtype) for i in range(count)]

        atoms = sb.tile([P, S // PER_COLUMN], U16, name="atoms")
        partners = sb.tile([P, S // PER_COLUMN], U16, name="partners")
        v_words = tiles("v_words", 2, [P, T], I32)
        v_scales = tile("v_scales", [P, T // I32_BYTES], I32)
        v2_words = tile("v2_words", [P, T], I32)
        v2_scales = tile("v2_scales", [P, T // I32_BYTES], I32)
        wb_words_in = tile("wb_words_in", [P, 2 * H // I32_BYTES], I32)
        wb_scales_in = tile("wb_scales_in", [P, H // I32_BYTES], I32)
        wb_words = tile("wb_words", [P, 2 * H], U8)
        wb_scales = tile("wb_scales", [P, H], U8)
        atom_words = tiles("atom_words", 2, [P, S], U32)
        atom_scales = tile("atom_scales", [P, S], U8)
        partner_scales = tile("partner_scales", [P, S], U8)
        wa_words = tiles("wa_words1", 2, [P, PASS], U32)
        first_words = {}
        wa_scales = [tiles("wa_scales%d" % b, 2, [P, PASS], U8) for b in range(2)]
        wm_scales = tiles("wm_scales", 2, [P, N], U8)
        g_rows = tiles("g_rows", 2 * PACK, [P, T], F32)
        h_rows = tiles("h_planes", 2, [P, PACK * S], F32)
        h_planes = [row[:].rearrange("p (t j) -> p t j", t=PACK) for row in h_rows]
        bias = tile("bias", [P, PACK], F32)

        g_view = gT.rearrange("(b p t) c -> b t p c", p=P, t=PACK)
        out_view = out.rearrange("(t p) j -> p t j", p=P)

        def round_copy(on_scalar, dst, src):
            if on_scalar:
                nc.scalar.activation(dst, src, ACT.Copy)
            else:
                nc.vector.tensor_copy(dst, src)

        def load_words(dst, src):
            nc.sync.dma_start(dst[:], src.rearrange("p c i -> p (c i)").bitcast(I32))

        def load_scales(dst, src, quads=()):
            rows = SCALE_ROWS * src.shape[0]
            if rows == SCALE_ROWS:
                for r in range(SCALE_ROWS):
                    nc.sync.dma_start(dst[r:P:QUADRANT, :], src[0, r::SCALE_ROWS, :].bitcast(I32))
                return
            for quad in quads:
                blocks = src[:, SCALE_ROWS * quad : SCALE_ROWS * (quad + 1), :]
                first_row = QUADRANT * quad + SCALE_ROWS
                queue = nc.sync if quad == 3 else nc.gpsimd
                queue.dma_start(dst[first_row : first_row + rows, :], blocks.bitcast(I32))

        def load_weight(slot, w, a, b):
            dst = tile("weight_in%d" % slot, [P, PACK, PASS], F32)
            piece = w[a * PASS : (a + 1) * PASS, b * PASS : (b + 1) * PASS]
            nc.sync.dma_start(dst[:], piece.rearrange("(p i) c -> p i c", i=PACK))
            return dst

        def load_g(b, t):
            nc.sync.dma_start(g_rows[PACK * b + t][:], g_view[b, t])

        def entries(lst, j):
            return lst[:, j.start // PER_COLUMN : j.stop // PER_COLUMN]

        def pick(dst, table, dtype, lst, j):
            nc.vector.tensor_copy(dst[:, j], table[:].bitcast(dtype).indirect(entries(lst, j)))

        def round_weight(slot, src, scalar_does):
            staged = tile("staged%d" % slot, [P, PACK * PASS], BF16)
            dst = staged[:].rearrange("p (t m i) -> p m i t", t=PACK, i=PACK)
            src = src[:].rearrange("p i (m t) -> p m i t", t=PACK)
            for on_scalar, t in zip(scalar_does, (slice(0, 2), slice(2, PACK))):
                round_copy(on_scalar, dst[:, :, :, t], src[:, :, :, t])
            return staged

        def quantize_weight(words, scales, staged):
            for part in range(2):
                c = slice(part * PASS // 2, (part + 1) * PASS // 2)
                quantize(words[:, c], scales[:, c], staged[:, PACK * c.start : PACK * c.stop])

        def interleave(dst, src, scalar_does):
            dst = dst.rearrange("p (run e t) -> p run t e", e=RUN, t=PACK)
            runs = src.shape[2] // RUN // len(scalar_does)
            src = src.rearrange("p t (run e) -> p run t e", e=RUN)
            for part, on_scalar in enumerate(scalar_does):
                round_copy(on_scalar, dst[:, part * runs : (part + 1) * runs], src[:, part * runs : (part + 1) * runs])

        def round_rows(name, src, scalar_does):
            staged = tile(name, [P, PACK * src.shape[2]], BF16)
            interleave(staged[:], src, scalar_does)
            return staged

        def quantize(words, scales, src):
            nc.vector.quantize_mx(out=words.bitcast(FP8X4), scales=scales, in_=src)

        def wa_columns(b, a, t):
            if b == 0:
                return first_words[a, t // 2][:, (t % 2) * P : (t % 2 + 1) * P]
            return wa_words[a][:, t * P : (t + 1) * P]

        def square_of_d(dst, b, t, half):
            bank = ps.tile([P, HALF], F32, name="bank%d" % (2 * (t % 2) + half))
            j, m = HALVES[half], slice(t * P, (t + 1) * P)
            r = b * PASS + t * P
            atom_passes = [
                (wa_columns(b, a, t).bitcast(FP8X4), wa_scales[b][a][:, m], atom_words[a], atom_scales[SCALE_ROWS * (a + 1) :, j])
                for a in range(2)
            ]
            partner_pass = [
                (wb_words[:, 2 * r : 2 * (r + P)].bitcast(FP4X4), wb_scales[:, r : r + P], partner_words, partner_scales[:, j])
            ]
            passes = atom_passes + partner_pass if b == 0 and t + half < 2 else partner_pass + atom_passes
            for i, (weight, weight_scales, words, scales) in enumerate(passes):
                nc.tensor.matmul_mx(
                    bank[:],
                    lhsT=weight,
                    lhsT_scale=weight_scales,
                    rhs=words[:, j].bitcast(FP8X4),
                    rhs_scale=scales,
                    start=(i == 0),
                    stop=(i == 2),
                )
            nc.scalar.activation(dst, bank[:], ACT.Square)

        def squares_of_pair(b, pair, order):
            squares = tiles("square", 2, [P, S], F32)
            for i, half in order:
                square_of_d(squares[i][:, HALVES[half]], b, 2 * pair + i, half)
            return squares

        def gaussian(name, square, j):
            plane = tile(name, [P, j.stop - j.start], F32)
            nc.scalar.activation(plane[:], square[:, j], ACT.Exp, scale=-1.0)
            return plane

        def weigh(factor, b, t, j):
            window = g_rows[PACK * b + t][:].indirect(entries(atoms, j))
            nc.vector.tensor_tensor(h_planes[b][:, t, j], window, factor, ALU.mult)

        def finish(name, bank, pair, j, on_scalar):
            result = tile(name, [P, 2, QUARTER], F32)
            if on_scalar:
                for i in range(2):
                    column = bias[:, 2 * pair + i : 2 * pair + i + 1]
                    nc.scalar.activation(result[:, i, :], bank[:, i, :], ACT.Identity, bias=column)
            else:
                columns = bias[:, 2 * pair : 2 * pair + 2].unsqueeze(2).to_broadcast([P, 2, QUARTER])
                nc.vector.tensor_tensor(result[:], bank[:], columns, ALU.add)
            nc.sync.dma_start(out_view[:, 2 * pair : 2 * pair + 2, j], result[:])

        VECTOR, SHARED = (False, False), (False, True)

        nc.gpsimd.memset(v_scales[:], 0)
        nc.vector.memset(v2_scales[:], 0)
        nc.vector.memset(wb_scales_in[:], 0)
        load_scales(v_scales, tab_scales, (0, 2, 1))

        nc.sync.dma_start(partners[:], offs2)
        nc.sync.dma_start(wb_words_in[:], wb4_words[0].bitcast(I32))
        load_scales(v2_scales, tab2_scales)
        nc.sync.dma_start(atoms[:], offs)
        load_words(v_words[0], tab_words[0])
        load_words(v_words[1], tab_words[1])
        load_scales(v_scales, tab_scales, (3,))
        load_scales(wb_scales_in, wb4_scales)
        wa00 = load_weight(0, wa, 0, 0)
        wa10 = load_weight(1, wa, 1, 0)
        load_words(v2_words, tab2_words[0])
        wa01 = load_weight(2, wa, 0, 1)
        load_g(0, 0)
        wa11 = load_weight(3, wa, 1, 1)

        half_pass = PASS // 2

        def round_pair(name, src, pair):
            staged = tile(name, [P, PACK * half_pass], BF16)
            dst = staged[:].rearrange("p (t m i) -> p m i t", t=2, i=PACK)
            round_copy(True, dst, src[:].rearrange("p i (m t) -> p m i t", t=PACK)[:, :, :, 2 * pair : 2 * pair + 2])
            return staged

        def quantize_pair(name, a, pair, staged):
            words = tile(name, [P, half_pass], U32)
            quantize(words[:], wa_scales[0][a][:, pair * half_pass : (pair + 1) * half_pass], staged[:])
            first_words[a, pair] = words

        nc.scalar.copy(
            wb_words[:].bitcast(U16).rearrange("p (b t m) -> p b t m", b=2, t=PACK),
            wb_words_in[:].bitcast(U16).rearrange("p (b m t) -> p b t m", b=2, t=PACK),
        )
        pick(partner_scales, v2_scales, U8, partners, WHOLE)
        pick(atom_words[0], v_words[0], U32, atoms, WHOLE)
        pick(atom_words[1], v_words[1], U32, atoms, WHOLE)
        nc.vector.tensor_copy(
            wb_scales[:].rearrange("p (b t m) -> p b t m", b=2, t=PACK),
            wb_scales_in[:].bitcast(U8).rearrange("p (b m t) -> p b t m", b=2, t=PACK),
        )
        pick(atom_scales, v_scales, U8, atoms, WHOLE)
        pieces = [round_pair("staged0", wa00, 0), round_pair("pair1", wa00, 1), round_pair("pair2", wa10, 0), round_pair("staged1", wa10, 1)]
        quantize_pair("v_scales", 0, 0, pieces[0])
        quantize_pair("wa_words001", 0, 1, pieces[1])
        quantize_pair("wa_words010", 1, 0, pieces[2])
        partner_words = tile("pair1", [P, S], U32)
        for j in HALVES:
            pick(partner_words, v2_words, U32, partners, j)

        for t in range(1, PACK):
            load_g(0, t)
        for t in range(PACK):
            load_g(1, t)
        wm0 = load_weight(0, wm, 0, 0)
        wm1 = load_weight(1, wm, 1, 0)
        with nc.allow_non_contiguous_dma(reason="one bias value for each partition and output tile"):
            nc.sync.dma_start(bias[:], bm.rearrange("(t p) -> p t", p=P))

        quantize_weight(wa_words[0], wa_scales[1][0], round_weight(2, wa01, VECTOR))
        quantize_pair("weight_in2", 1, 1, pieces[3])
        first = tile("gauss0", [P, S], F32)
        squares = tiles("square", 2, [P, S], F32)
        for half, j in enumerate(HALVES):
            for t in range(2):
                square_of_d(squares[t][:, j], 0, t, half)
            nc.scalar.activation(first[:, j], squares[0][:, j], ACT.Exp, scale=-1.0)
        second = gaussian("gauss1", squares[1], WHOLE)
        for j in HALVES:
            weigh(first[:, j], 0, 0, j)
        quantize_weight(wa_words[1], wa_scales[1][1], round_weight(3, wa11, VECTOR))
        weigh(second[:], 0, 1, WHOLE)
        by_plane = [(i, half) for i in range(2) for half in range(2)]
        for i, square in enumerate(squares_of_pair(0, 1, by_plane)):
            weigh(gaussian("gauss%d" % (2 + i), square, WHOLE)[:], 0, 2 + i, WHOLE)

        quarters = [slice(q * QUARTER, (q + 1) * QUARTER) for q in range(4)]
        late = [gaussian("v_words%d" % i, square, WHOLE) for i, square in enumerate(squares_of_pair(1, 0, by_plane))]
        squares = squares_of_pair(1, 1, by_plane)
        late.append(gaussian("v2_words", squares[0], WHOLE))
        last_first = gaussian("gauss0", squares[1], quarters[0])
        last_second = gaussian("gauss1", squares[1], quarters[1])
        last_rest = gaussian("gauss2", squares[1], HALVES[1])
        h0_first = round_rows("staged0", h_planes[0][:, :, HALVES[0]], (True,))
        eighth = QUARTER // 2
        h0_second = tile("staged3", [P, PACK * HALF], BF16)
        interleave(h0_second[:], h_planes[0][:, :, HALVES[1]], (True,))
        h0_third, h0_fourth = h0_second[:, 0 : PACK * QUARTER], h0_second[:, PACK * QUARTER : PACK * HALF]

        def mx_tiles(name, columns, words_name=None):
            return tile(words_name or name + "_words", [P, columns], U32), tile(name + "_scales", [P, columns], U8)

        def round_quarter(staged, q, on_scalar):
            dst = staged[:, PACK * QUARTER * (q % 2) : PACK * QUARTER * (q % 2 + 1)]
            interleave(dst, h_planes[1][:, :, quarters[q]], (on_scalar,))
            return dst

        for t in range(PACK - 1):
            weigh(late[t][:], 1, t, WHOLE)
        weigh(last_first[:], 1, PACK - 1, quarters[0])
        weigh(last_second[:], 1, PACK - 1, quarters[1])
        h1_first = tile("staged1", [P, PACK * HALF], BF16)
        rounded = [round_quarter(h1_first, q, True) for q in range(2)]
        h0_words, h0_scales = mx_tiles("h0_first", HALF, "gauss0")
        quantize(h0_words[:], h0_scales[:], h0_first[:])
        idle_bank = ps.tile([P, HALF], F32, name="bank0")
        for unused in range(4):
            nc.tensor.matmul_mx(
                idle_bank[:],
                lhsT=wa_words[1][:, 0:P].bitcast(FP8X4),
                lhsT_scale=wa_scales[1][1][:, 0:P],
                rhs=h0_words[:].bitcast(FP8X4),
                rhs_scale=h0_scales[:],
                start=True,
                stop=True,
            )
        weigh(last_rest[:, quarters[0]], 1, PACK - 1, quarters[2])
        late_words, late_scales = mx_tiles("h0_second", HALF, "gauss1")
        quantize(late_words[:, quarters[0]], late_scales[:, quarters[0]], h0_third)
        h1_words, h1_scales = mx_tiles("h1_first", HALF)
        quantize(h1_words[:, quarters[0]], h1_scales[:, quarters[0]], rounded[0])
        first_pair, second_pair = slice(0, 2 * P), slice(2 * P, N)
        wm0_rounded = round_rows("staged2", wm0[:], SHARED)
        wm0_staged = [wm0_rounded[:, 0 : PACK * 2 * P], wm0_rounded[:, PACK * 2 * P :]]
        quantize(h1_words[:, quarters[1]], h1_scales[:, quarters[1]], rounded[1])
        wm0_first = tile("wm_words0", [P, 2 * P], U32)
        quantize(wm0_first[:], wm_scales[0][:, first_pair], wm0_staged[0])
        third_end = tile("staged0", [P, PACK * eighth], BF16)
        wm1_pieces = [
            (third_end[:, 0 : PACK * P // 2], slice(0, P // 2)),
            (tile("square1", [P, PACK * P // 2], BF16)[:], slice(P // 2, P)),
            (h_rows[1][:, PACK * S - QUARTER :].bitcast(BF16), slice(P, 2 * P)),
        ]
        wm1_words = tile("wm_words1", [P, N], U32)
        for staged, c in wm1_pieces:
            interleave(staged, wm1[:, :, c], (False,))
        wm1_second = round_rows("square0", wm1[:, :, second_pair], (True,))
        for staged, c in wm1_pieces:
            quantize(wm1_words[:, c], wm_scales[1][:, c], staged)
        interleave(third_end[:], h_planes[1][:, :, HALF + eighth : HALF + QUARTER], (True,))
        wm0_second = tile("square1", [P, 2 * P], U32)
        quantize(wm0_second[:], wm_scales[0][:, second_pair], wm0_staged[1])
        weigh(last_rest[:, quarters[1]], 1, PACK - 1, quarters[3])
        quantize(wm1_words[:, second_pair], wm_scales[1][:, second_pair], wm1_second[:])
        wm_words = [[wm0_first[:], wm0_second[:]], [wm1_words[:, first_pair], wm1_words[:, second_pair]]]

        def message_pass(bank, b, t, words, scales, start, stop):
            m = slice(t * P, (t + 1) * P)
            nc.tensor.matmul_mx(
                bank,
                lhsT=wm_words[b][t // 2][:, (t % 2) * P : (t % 2 + 1) * P].bitcast(FP8X4),
                lhsT_scale=wm_scales[b][:, m],
                rhs=words.bitcast(FP8X4),
                rhs_scale=scales,
                start=start,
                stop=stop,
            )

        for t in range(PACK):
            bank = ps.tile([P, HALF], F32, name="bank%d" % (PACK + t))
            message_pass(bank[:], 0, t, h0_words[:], h0_scales[:], True, False)
            message_pass(bank[:], 1, t, h1_words[:], h1_scales[:], False, True)
            result = tile("g_rows%d" % t, [P, HALF], F32)
            nc.scalar.activation(result[:], bank[:], ACT.Identity, bias=bias[:, t : t + 1])
            nc.sync.dma_start(out_view[:, t, HALVES[0]], result[:])

        third_start = round_rows("staged2", h_planes[1][:, :, HALF : HALF + eighth], (False,))
        fourth_words = tile("gauss2", [P, QUARTER], U32)
        quantize(fourth_words[:], late_scales[:, quarters[1]], h0_fourth)
        sums = [[ps.tile([P, 2, QUARTER], F32, name="bank%d" % (2 * q + pair)) for pair in range(2)] for q in range(2)]

        def quarter_pass(q, b, words, scales):
            for i in range(2):
                for pair in range(2):
                    message_pass(sums[q][pair][:, i, :], b, 2 * pair + i, words, scales, (b, i) == (0, 0), (b, i) == (1, 1))

        for q in range(2):
            quarter_pass(q, 0, (late_words[:, quarters[0]], fourth_words[:])[q], late_scales[:, quarters[q]])
            if q == 0:
                rounded = (third_end[:], third_start[:])
            else:
                fourth = round_rows("staged1", h_planes[1][:, :, quarters[3]], VECTOR)
                rounded = (fourth[:, PACK * eighth :], fourth[:, 0 : PACK * eighth])
            words, scales = mx_tiles("h1_quarter%d" % q, QUARTER)
            for staged, c in zip(rounded[:: 1 - 2 * q], (slice(eighth, QUARTER), slice(0, eighth))[:: 1 - 2 * q]):
                quantize(words[:, c], scales[:, c], staged)
            quarter_pass(q, 1, words[:], scales[:])
            for pair in range(2):
                finish("g_rows%d" % (PACK + 2 * q + pair), sums[q][pair], pair, quarters[2 + q], pair == 0)
